import numpy as np
import ml_dtypes


def mxq(x, axis, fmt="e4m3"):
    dtype, down = {"e4m3": (ml_dtypes.float8_e4m3fn, 7), "e5m2": (ml_dtypes.float8_e5m2, 14)}[fmt]
    v = np.moveaxis(np.asarray(x, np.float32).astype(ml_dtypes.bfloat16).astype(np.float64), axis, -1)
    blocks = v.reshape(v.shape[:-1] + (-1, 32))
    amax = np.abs(blocks).max(-1, keepdims=True)
    byte = np.maximum(np.where(amax > 0, np.frexp(amax)[1] - 1 + 127, 0) - down, 1)
    scale = np.exp2(byte - 127.0)
    codes = (blocks / scale).astype(np.float32).astype(dtype).astype(np.float64)
    return np.moveaxis((codes * scale).reshape(v.shape), -1, axis)


WIDE = False


def mx_kscale(k):
    if not WIDE:
        return np.ones(k)
    levels = np.array([10, -10, 5, -5, 0])
    if k % 512:
        return np.exp2(np.random.permutation(np.resize(levels, k // 32))).repeat(32)
    a = np.empty((k // 512, 16))
    for p in range(k // 512):
        a[p, :8] = np.random.permutation(np.resize(levels, 8))
        for g in range(8):
            far = levels[np.abs(levels - a[p, g]) >= 10]
            a[p, g + 8] = far[np.random.randint(len(far))]
    return np.exp2(a.ravel()).repeat(32)


def f64(x):
    return np.asarray(x).astype(np.float64)


def striped(idx):
    return np.tile(idx.reshape(-1, 16).T, (8, 1)).astype(np.uint16)


def unstriped(offs):
    return offs[:16].T.reshape(-1).astype(np.int64)


E2M1 = np.array([0.0, 0.5, 1.0, 1.5, 2.0, 3.0, 4.0, 6.0, -0.0, -0.5, -1.0, -1.5, -2.0, -3.0, -4.0, -6.0])


def pack_weight(w, fmt):
    k, n = w.shape
    w = f64(np.asarray(w, np.float32).astype(ml_dtypes.bfloat16)).reshape(k // 32, 32, n)
    amax = np.abs(w).max(1)
    if fmt == "e4m3":
        byte = np.frexp(amax)[1] - 1 + 127 - 7
    else:
        mant, ex = np.frexp(amax / 6.0)
        byte = np.where(mant > 0.5, ex, ex - 1) + 127
    byte = np.clip(np.where(amax > 0, byte, 1), 1, 254)
    scaled = (w * np.exp2(127.0 - byte)[:, None, :]).reshape(k, n).astype(np.float32)
    by_word = np.ascontiguousarray(scaled.reshape(k // 512, 128, 4, n).transpose(0, 1, 3, 2))
    if fmt == "e4m3":
        words = by_word.astype(ml_dtypes.float8_e4m3fn).view(np.uint8)
    else:
        c = by_word.astype(ml_dtypes.float4_e2m1fn).view(np.uint8) & 0xF
        words = (c[..., 0::2] | (c[..., 1::2] << 4)).reshape(k // 512, 128, 2 * n)
    return np.ascontiguousarray(words), np.ascontiguousarray(byte.astype(np.uint8).reshape(k // 512, 16, n))


def unpack_weight(words, scales, fmt):
    g, _, n = scales.shape
    words = np.ascontiguousarray(words).reshape(g, 128, n, -1)
    if fmt == "e4m3":
        vals = words.view(ml_dtypes.float8_e4m3fn).astype(np.float64)
    else:
        nib = np.empty((g, 128, n, 4), np.uint8)
        nib[..., 0::2] = words & 0xF
        nib[..., 1::2] = words >> 4
        vals = E2M1[nib]
    vals = vals * np.repeat(np.exp2(scales.astype(np.float64) - 127.0), 8, axis=1)[..., None]
    return vals.transpose(0, 1, 3, 2).reshape(g * 512, n)


def d_relu2(v):
    return 2.0 * np.maximum(v, 0.0)


K, T, E, C, H, N = 512, 512, 2, 256, 512, 1024


def by_expert(wq, xq):
    return np.concatenate([wq[e].T @ xq[:, e * C:(e + 1) * C] for e in range(E)], axis=1)


def setup_inputs():
    n = np.random.standard_normal
    v = mx_kscale(N)
    u = mx_kscale(H)
    slot_token = np.random.permutation(T)[:E * C]
    w_slot = np.random.uniform(0.2, 1.0, E * C)
    partner = np.random.permutation(T)[:E * C]
    dy = pack_weight(n((N, T)) * v[:, None], "e4m3")
    w2t = [pack_weight(m, "e4m3") for m in n((E, N, H)) / np.sqrt(N) / v[None, :, None] * u]
    w1t = [pack_weight(m, "e4m3") for m in n((E, H, K)) / np.sqrt(H) / u[None, :, None]]
    wpt = [pack_weight(m, "e2m1") for m in n((E, H, K)) / np.sqrt(H) / u[None, :, None]]
    return {
        "dy_words": dy[0],
        "dy_scales": dy[1],
        "w2t_words": np.stack([m[0] for m in w2t]),
        "w2t_scales": np.stack([m[1] for m in w2t]),
        "w1t_words": np.stack([m[0] for m in w1t]),
        "w1t_scales": np.stack([m[1] for m in w1t]),
        "wpt_words": np.stack([m[0] for m in wpt]),
        "wpt_scales": np.stack([m[1] for m in wpt]),
        "a": (n((H, E * C))).astype(np.float32),
        "gate": (np.tile(w_slot, (128, 1))).astype(np.float32),
        "offs": striped(slot_token),
        "offs2": striped(partner),
    }


def reference(dy_words, dy_scales, w2t_words, w2t_scales, w1t_words, w1t_scales, wpt_words, wpt_scales, a, gate, offs, offs2):
    w2t = np.stack([unpack_weight(w2t_words[e], w2t_scales[e], "e4m3") for e in range(E)])
    w1t = np.stack([unpack_weight(w1t_words[e], w1t_scales[e], "e4m3") for e in range(E)])
    wpt = np.stack([unpack_weight(wpt_words[e], wpt_scales[e], "e2m1") for e in range(E)])
    idx, idx2 = unstriped(offs), unstriped(offs2)
    gq = unpack_weight(dy_words, dy_scales, "e4m3")[:, idx]
    dh = f64(gate[:1]) * by_expert(w2t, gq) * d_relu2(f64(a))
    dq = mxq(dh, 0, "e4m3")
    out = np.zeros((K, T))
    out[:, idx] = by_expert(w1t, dq)
    out[:, idx2] += by_expert(wpt, dq)
    return out

@@ -1,0 +1,205 @@
+from contextlib import ExitStack
+
+import concourse.mybir as mybir
+from concourse.masks import make_identity
+
+K, T, E, C, H, N = 512, 512, 2, 256, 512, 1024
+SLOTS = E * C
+FLOPS = 2 * SLOTS * H * (N + 2 * K)
+
+F32 = mybir.dt.float32
+BF16 = mybir.dt.bfloat16
+I32 = mybir.dt.int32
+U32 = mybir.dt.uint32
+U16 = mybir.dt.uint16
+U8 = mybir.dt.uint8
+FP8X4 = mybir.dt.float8_e4m3fn_x4
+FP4X4 = mybir.dt.float4_e2m1fn_x4
+COPY = mybir.ActivationFunctionType.Copy
+RELU = mybir.ActivationFunctionType.Relu
+MULT = mybir.AluOpType.mult
+ADD = mybir.AluOpType.add
+
+P = 128
+PACK = 4
+PASSES = N // (P * PACK)
+CHUNKS = SLOTS // P
+K_TILES = K // P
+PER_COL = 16
+WINDOW = 768
+
+
+def tile_moe_dub_relu2_kernel(
+    tc, dy_words, dy_scales, w2t_words, w2t_scales, w1t_words, w1t_scales, wpt_words, wpt_scales, a, gate, offs, offs2, out
+):
+    nc = tc.nc
+    with ExitStack() as ctx:
+        keep = ctx.enter_context(tc.tile_pool(name="keep", bufs=1))
+        sums_psum = ctx.enter_context(tc.psum_pool(name="sums_psum", bufs=2))
+        turned_psum = ctx.enter_context(tc.psum_pool(name="turned_psum", bufs=2))
+        grad_psum = ctx.enter_context(tc.psum_pool(name="grad_psum", bufs=4))
+
+        own_list = keep.tile([P, SLOTS // PER_COL], U16, name="own_list")
+        partner_list = keep.tile([P, SLOTS // PER_COL], U16, name="partner_list")
+        dy_codes = [keep.tile([P, T], I32, name=f"dy_codes{s}", align_bytes=64) for s in range(PASSES)]
+        dy_bytes = keep.tile([P, T], U8, name="dy_bytes", align_bytes=64)
+        w2_codes = [keep.tile([P, PASSES, H], I32, name=f"w2_codes{e}", align_bytes=64) for e in range(E)]
+        w2_bytes = keep.tile([P, H], U8, name="w2_bytes", align_bytes=64)
+        w1_codes = [keep.tile([P, K], I32, name=f"w1_codes{e}", align_bytes=64) for e in range(E)]
+        w1_bytes = keep.tile([P, K], U8, name="w1_bytes", align_bytes=64)
+        wp_codes = keep.tile([P, E, 2 * K], U8, name="wp_codes", align_bytes=64)
+        wp_bytes = keep.tile([P, E, K], U8, name="wp_bytes", align_bytes=64)
+        saved = [keep.tile([P, PACK, C], F32, name=f"saved{e}", align_bytes=64) for e in range(E)]
+        gate_col = keep.tile([P, CHUNKS], F32, name="gate_col")
+        ones_diagonal = keep.tile([P, P], F32, name="ones_diagonal", align_bytes=64)
+        identity = keep.tile([P, P], F32, name="identity", align_bytes=64)
+
+        for plane in (dy_bytes, w2_bytes, w1_bytes):
+            nc.vector.memset(plane[:].bitcast(I32), 0)
+        nc.vector.memset(wp_bytes[:].rearrange("p e k -> p (e k)").bitcast(I32), 0)
+        make_identity(nc, ones_diagonal[:])
+        nc.scalar.activation(out=identity[:], in_=ones_diagonal[:], func=RELU)
+
+        def load_planes(queue, plane, rows):
+            count = rows.shape[0]
+            for q in range(4):
+                queue.dma_start(
+                    out=plane[32 * q : 32 * q + 4 * count, :].bitcast(I32),
+                    in_=rows[:, 4 * q : 4 * q + 4, :].bitcast(I32),
+                )
+
+        def load_w2(e):
+            nc.sync.dma_start(out=w2_codes[e][:], in_=w2t_words[e].rearrange("s p i d -> p s (i d)").bitcast(I32))
+
+        def load_saved(e):
+            nc.sync.dma_start(out=saved[e][:], in_=a[:, e * C : (e + 1) * C].rearrange("(p t) j -> p t j", t=PACK))
+
+        def load_w1(e):
+            nc.sync.dma_start(out=w1_codes[e][:], in_=w1t_words[e].rearrange("s p k d -> p (s k d)").bitcast(I32))
+
+        nc.sync.dma_start(own_list[:], offs)
+        for s in range(PASSES):
+            nc.sync.dma_start(out=dy_codes[s][:], in_=dy_words[s].rearrange("p t d -> p (t d)").bitcast(I32))
+        load_planes(nc.sync, dy_bytes, dy_scales)
+        load_w2(0)
+        load_planes(nc.sync, w2_bytes, w2t_scales.rearrange("e s b i -> (e s) b i"))
+        with nc.allow_non_contiguous_dma(reason="one gate value a partition and chunk"):
+            nc.sync.dma_start(out=gate_col[:], in_=gate[0:1, :].rearrange("o (c p) -> p (o c)", p=P))
+        load_saved(0)
+        load_w2(1)
+        load_saved(1)
+        load_planes(nc.sync, w1_bytes, w1t_scales.rearrange("e s b k -> (e s) b k"))
+        load_w1(0)
+        nc.sync.dma_start(out=wp_codes[:].bitcast(I32), in_=wpt_words.rearrange("e s p b -> p (e s) b").bitcast(I32))
+        load_w1(1)
+        nc.sync.dma_start(partner_list[:], offs2)
+        wp_rows = wpt_scales.rearrange("e s b k -> b (e s) k")
+        for q in range(4):
+            nc.gpsimd.dma_start(
+                out=wp_bytes[32 * q : 32 * q + 4, :, :].bitcast(I32),
+                in_=wp_rows[4 * q : 4 * q + 4, :, :].bitcast(I32),
+            )
+
+        def list_cols(first, count):
+            return slice(first // PER_COL, (first + count) // PER_COL)
+
+        g_codes, g_bytes = {}, {}
+        for e in range(E):
+            picks = own_list[:, list_cols(e * C, C)]
+            for s in range(PASSES):
+                g_codes[e, s] = keep.tile([P, C], U32, name=f"g_codes{e}{s}", align_bytes=64)
+                nc.vector.tensor_copy(g_codes[e, s][:], dy_codes[s][:].bitcast(U32).indirect(picks))
+            g_bytes[e] = keep.tile([P, C], U8, name=f"g_bytes{e}", align_bytes=64)
+            nc.vector.tensor_copy(g_bytes[e][:], dy_bytes[:].indirect(picks))
+
+        dh = [keep.tile([P, C * PACK], BF16, name=f"dh{e}", align_bytes=64) for e in range(E)]
+        dh_codes = [keep.tile([P, C], U32, name=f"dh_codes{e}", align_bytes=64) for e in range(E)]
+        dh_bytes = [keep.tile([P, C], U8, name=f"dh_bytes{e}", align_bytes=64) for e in range(E)]
+
+        def hidden_gradient(c):
+            e, half = divmod(c, C // P)
+            cols = slice(half * P, (half + 1) * P)
+            slope = keep.tile([P, P * PACK], F32, name=f"slope{c}", align_bytes=64)
+            nc.scalar.activation(
+                out=slope[:].rearrange("p (u v t) -> p u t v", v=2, t=PACK),
+                in_=saved[e][:, :, cols].rearrange("p t (u v) -> p u t v", v=2),
+                func=RELU,
+                scale=2.0,
+            )
+            sums = sums_psum.tile([P, H], F32, name="sums")
+            for s in range(PASSES):
+                nc.tensor.matmul_mx(
+                    out=sums[:],
+                    lhsT=g_codes[e, s][:, cols].bitcast(FP8X4),
+                    lhsT_scale=g_bytes[e][4 * s :, cols],
+                    rhs=w2_codes[e][:, s, :].bitcast(FP8X4),
+                    rhs_scale=w2_bytes[4 * (PASSES * e + s) :, :],
+                    start=(s == 0),
+                    stop=(s == PASSES - 1),
+                )
+            gated = keep.tile([P, PACK, P], F32, name=f"gated{c}", align_bytes=64)
+            nc.scalar.activation(
+                out=gated[:], in_=sums[:].rearrange("j (m t) -> j t m", t=PACK), func=COPY, scale=gate_col[:, c : c + 1]
+            )
+            turned = turned_psum.tile([P, PACK, P], F32, name="turned")
+            for t in range(PACK):
+                nc.tensor.transpose(turned[:, t, :], gated[:, t, :], identity[:])
+            nc.vector.tensor_tensor(
+                out=dh[e][:, half * P * PACK : (half + 1) * P * PACK].rearrange("p (j t) -> p j t", t=PACK),
+                in0=turned[:].rearrange("p t j -> p j t"),
+                in1=slope[:].rearrange("p (j t) -> p j t", t=PACK),
+                op=MULT,
+            )
+
+        def quantise(e):
+            nc.vector.quantize_mx(out=dh_codes[e][:].bitcast(FP8X4), scales=dh_bytes[e][:], in_=dh[e][:])
+
+        by_slot = [keep.tile([P, 2, SLOTS], F32, name=f"by_slot{kt}", align_bytes=64) for kt in range(K_TILES)]
+
+        def token_gradients(kt, e):
+            rows = slice(kt * P, (kt + 1) * P)
+            grads = grad_psum.tile([P, 2, C], F32, name="grads")
+            nc.tensor.matmul_mx(
+                out=grads[:, 0, :],
+                lhsT=w1_codes[e][:, rows].bitcast(FP8X4),
+                lhsT_scale=w1_bytes[4 * e :, rows],
+                rhs=dh_codes[e][:].bitcast(FP8X4),
+                rhs_scale=dh_bytes[e][:],
+                start=True,
+                stop=True,
+            )
+            nc.tensor.matmul_mx(
+                out=grads[:, 1, :],
+                lhsT=wp_codes[:, e, 2 * kt * P : 2 * (kt + 1) * P].bitcast(FP4X4),
+                lhsT_scale=wp_bytes[:, e, rows],
+                rhs=dh_codes[e][:].bitcast(FP8X4),
+                rhs_scale=dh_bytes[e][:],
+                start=True,
+                stop=True,
+            )
+            nc.scalar.copy(out=by_slot[kt][:, :, e * C : (e + 1) * C], in_=grads[:])
+
+        hidden_gradient(0)
+        hidden_gradient(1)
+        quantise(0)
+        hidden_gradient(2)
+        hidden_gradient(3)
+        token_gradients(0, 0)
+        quantise(1)
+        token_gradients(0, 1)
+        for kt in range(1, K_TILES):
+            for e in range(E):
+                token_gradients(kt, e)
+
+        for kt in range(K_TILES):
+            own = keep.tile([P, WINDOW], F32, name=f"own{kt}", align_bytes=64)
+            partner = keep.tile([P, WINDOW], F32, name=f"partner{kt}", align_bytes=64)
+            pieces = [(e * C, C) for e in range(E)] if kt == 0 else [(0, SLOTS)]
+            for first, count in pieces:
+                for m, (window, offsets) in enumerate(((own, own_list), (partner, partner_list))):
+                    nc.vector.tensor_copy(
+                        window[:].indirect(offsets[:, list_cols(first, count)]), by_slot[kt][:, m, first : first + count]
+                    )
+            total = keep.tile([P, T], F32, name=f"total{kt}", align_bytes=64)
+            nc.vector.tensor_tensor(total[:], own[:, :T], partner[:, :T], ADD)
+            nc.sync.dma_start(out=out[kt * P : (kt + 1) * P, :], in_=total[:])

@@ -45,7 +45,7 @@ def tile_moe_dub_relu2_kernel(
         dy_bytes = keep.tile([P, T], U8, name="dy_bytes", align_bytes=64)
         w2_codes = [keep.tile([P, PASSES, H], I32, name=f"w2_codes{e}", align_bytes=64) for e in range(E)]
         w2_bytes = keep.tile([P, H], U8, name="w2_bytes", align_bytes=64)
-        w1_codes = [keep.tile([P, K], I32, name=f"w1_codes{e}", align_bytes=64) for e in range(E)]
+        w1_codes = keep.tile([P, E, K], I32, name="w1_codes", align_bytes=64)
         w1_bytes = keep.tile([P, K], U8, name="w1_bytes", align_bytes=64)
         wp_codes = keep.tile([P, E, 2 * K], U8, name="wp_codes", align_bytes=64)
         wp_bytes = keep.tile([P, E, K], U8, name="wp_bytes", align_bytes=64)
@@ -58,7 +58,6 @@ def tile_moe_dub_relu2_kernel(
             nc.vector.memset(plane[:].bitcast(I32), 0)
         nc.vector.memset(wp_bytes[:].rearrange("p e k -> p (e k)").bitcast(I32), 0)
         make_identity(nc, ones_diagonal[:])
-        nc.scalar.activation(out=identity[:], in_=ones_diagonal[:], func=RELU)
 
         def load_planes(queue, plane, rows):
             count = rows.shape[0]
@@ -74,43 +73,40 @@ def tile_moe_dub_relu2_kernel(
         def load_saved(e):
             nc.sync.dma_start(out=saved[e][:], in_=a[:, e * C : (e + 1) * C].rearrange("(p t) j -> p t j", t=PACK))
 
-        def load_w1(e):
-            nc.sync.dma_start(out=w1_codes[e][:], in_=w1t_words[e].rearrange("s p k d -> p (s k d)").bitcast(I32))
-
+        nc.sync.dma_start(out=dy_codes[0][:], in_=dy_words[0].rearrange("p t d -> p (t d)").bitcast(I32))
         nc.sync.dma_start(own_list[:], offs)
-        for s in range(PASSES):
-            nc.sync.dma_start(out=dy_codes[s][:], in_=dy_words[s].rearrange("p t d -> p (t d)").bitcast(I32))
-        load_planes(nc.sync, dy_bytes, dy_scales)
+        nc.sync.dma_start(out=dy_codes[1][:], in_=dy_words[1].rearrange("p t d -> p (t d)").bitcast(I32))
+        load_planes(nc.scalar, dy_bytes, dy_scales)
         load_w2(0)
-        load_planes(nc.sync, w2_bytes, w2t_scales.rearrange("e s b i -> (e s) b i"))
+        load_planes(nc.scalar, w2_bytes, w2t_scales.rearrange("e s b i -> (e s) b i"))
         with nc.allow_non_contiguous_dma(reason="one gate value a partition and chunk"):
             nc.sync.dma_start(out=gate_col[:], in_=gate[0:1, :].rearrange("o (c p) -> p (o c)", p=P))
         load_saved(0)
         load_w2(1)
         load_saved(1)
         load_planes(nc.sync, w1_bytes, w1t_scales.rearrange("e s b k -> (e s) b k"))
-        load_w1(0)
-        nc.sync.dma_start(out=wp_codes[:].bitcast(I32), in_=wpt_words.rearrange("e s p b -> p (e s) b").bitcast(I32))
-        load_w1(1)
+        nc.sync.dma_start(out=w1_codes[:], in_=w1t_words.rearrange("e s p k d -> p (e s) (k d)").bitcast(I32))
         nc.sync.dma_start(partner_list[:], offs2)
         wp_rows = wpt_scales.rearrange("e s b k -> b (e s) k")
         for q in range(4):
-            nc.gpsimd.dma_start(
+            nc.sync.dma_start(
                 out=wp_bytes[32 * q : 32 * q + 4, :, :].bitcast(I32),
                 in_=wp_rows[4 * q : 4 * q + 4, :, :].bitcast(I32),
             )
+        nc.sync.dma_start(out=wp_codes[:].bitcast(I32), in_=wpt_words.rearrange("e s p b -> p (e s) b").bitcast(I32))
+        nc.scalar.activation(out=identity[:], in_=ones_diagonal[:], func=RELU)
 
         def list_cols(first, count):
             return slice(first // PER_COL, (first + count) // PER_COL)
 
-        g_codes, g_bytes = {}, {}
-        for e in range(E):
-            picks = own_list[:, list_cols(e * C, C)]
+        g_codes = [[keep.tile([P, C], U32, name=f"g_codes{e}{s}", align_bytes=64) for s in range(PASSES)] for e in range(E)]
+        g_bytes = [keep.tile([P, C], U8, name=f"g_bytes{e}", align_bytes=64) for e in range(E)]
+        for first, count in ((0, P), (P, P), (C, C)):
+            e, place = divmod(first, C)
+            picks = own_list[:, list_cols(first, count)]
             for s in range(PASSES):
-                g_codes[e, s] = keep.tile([P, C], U32, name=f"g_codes{e}{s}", align_bytes=64)
-                nc.vector.tensor_copy(g_codes[e, s][:], dy_codes[s][:].bitcast(U32).indirect(picks))
-            g_bytes[e] = keep.tile([P, C], U8, name=f"g_bytes{e}", align_bytes=64)
-            nc.vector.tensor_copy(g_bytes[e][:], dy_bytes[:].indirect(picks))
+                nc.vector.tensor_copy(g_codes[e][s][:, place : place + count], dy_codes[s][:].bitcast(U32).indirect(picks))
+            nc.vector.tensor_copy(g_bytes[e][:, place : place + count], dy_bytes[:].indirect(picks))
 
         dh = [keep.tile([P, C * PACK], BF16, name=f"dh{e}", align_bytes=64) for e in range(E)]
         dh_codes = [keep.tile([P, C], U32, name=f"dh_codes{e}", align_bytes=64) for e in range(E)]
@@ -130,7 +126,7 @@ def tile_moe_dub_relu2_kernel(
             for s in range(PASSES):
                 nc.tensor.matmul_mx(
                     out=sums[:],
-                    lhsT=g_codes[e, s][:, cols].bitcast(FP8X4),
+                    lhsT=g_codes[e][s][:, cols].bitcast(FP8X4),
                     lhsT_scale=g_bytes[e][4 * s :, cols],
                     rhs=w2_codes[e][:, s, :].bitcast(FP8X4),
                     rhs_scale=w2_bytes[4 * (PASSES * e + s) :, :],
@@ -156,18 +152,22 @@ def tile_moe_dub_relu2_kernel(
 
         by_slot = [keep.tile([P, 2, SLOTS], F32, name=f"by_slot{kt}", align_bytes=64) for kt in range(K_TILES)]
 
-        def token_gradients(kt, e):
+        def token_gradients(kt, e, apart):
             rows = slice(kt * P, (kt + 1) * P)
+            slots = slice(e * C, (e + 1) * C)
             grads = grad_psum.tile([P, 2, C], F32, name="grads")
             nc.tensor.matmul_mx(
                 out=grads[:, 0, :],
-                lhsT=w1_codes[e][:, rows].bitcast(FP8X4),
+                lhsT=w1_codes[:, e, rows].bitcast(FP8X4),
                 lhsT_scale=w1_bytes[4 * e :, rows],
                 rhs=dh_codes[e][:].bitcast(FP8X4),
                 rhs_scale=dh_bytes[e][:],
                 start=True,
                 stop=True,
             )
+            if apart:
+                nc.scalar.copy(out=by_slot[kt][:, 0, slots], in_=grads[:, 0, :])
+                grads = grad_psum.tile([P, 2, C], F32, name="grads")
             nc.tensor.matmul_mx(
                 out=grads[:, 1, :],
                 lhsT=wp_codes[:, e, 2 * kt * P : 2 * (kt + 1) * P].bitcast(FP4X4),
@@ -177,19 +177,22 @@ def tile_moe_dub_relu2_kernel(
                 start=True,
                 stop=True,
             )
-            nc.scalar.copy(out=by_slot[kt][:, :, e * C : (e + 1) * C], in_=grads[:])
+            if apart:
+                nc.scalar.copy(out=by_slot[kt][:, 1, slots], in_=grads[:, 1, :])
+            else:
+                nc.scalar.copy(out=by_slot[kt][:, :, slots], in_=grads[:])
 
         hidden_gradient(0)
         hidden_gradient(1)
         quantise(0)
+        token_gradients(0, 0, True)
         hidden_gradient(2)
         hidden_gradient(3)
-        token_gradients(0, 0)
         quantise(1)
-        token_gradients(0, 1)
+        token_gradients(0, 1, False)
         for kt in range(1, K_TILES):
             for e in range(E):
-                token_gradients(kt, e)
+                token_gradients(kt, e, False)
 
         for kt in range(K_TILES):
             own = keep.tile([P, WINDOW], F32, name=f"own{kt}", align_bytes=64)
@@ -201,5 +204,24 @@ def tile_moe_dub_relu2_kernel(
                         window[:].indirect(offsets[:, list_cols(first, count)]), by_slot[kt][:, m, first : first + count]
                     )
             total = keep.tile([P, T], F32, name=f"total{kt}", align_bytes=64)
-            nc.vector.tensor_tensor(total[:], own[:, :T], partner[:, :T], ADD)
-            nc.sync.dma_start(out=out[kt * P : (kt + 1) * P, :], in_=total[:])
+            rows = slice(kt * P, (kt + 1) * P)
+            if kt < K_TILES - 1:
+                summed = turned_psum.tile([P, PACK, P], F32, name="turned")
+                for b in range(T // P):
+                    for m, window in enumerate((own, partner)):
+                        nc.tensor.matmul(
+                            summed[:, b, :], window[:, b * P : (b + 1) * P], identity[:],
+                            start=(m == 0), stop=(m == 1), is_transpose=True,
+                        )
+                by_token = keep.tile([P, T // P, P], F32, name=f"by_token{kt}", align_bytes=64)
+                nc.scalar.copy(out=by_token[:], in_=summed[:])
+                back = turned_psum.tile([P, PACK, P], F32, name="turned")
+                for b in range(T // P):
+                    nc.tensor.transpose(back[:, b, :], by_token[:, b, :], identity[:])
+                nc.scalar.copy(out=total[:], in_=back[:].rearrange("p b t -> p (b t)"))
+                nc.scalar.dma_start(out=out[rows, :], in_=total[:])
+            else:
+                for half in range(2):
+                    cols = slice(half * T // 2, (half + 1) * T // 2)
+                    nc.vector.tensor_tensor(total[:, cols], own[:, cols], partner[:, cols], ADD)
+                    nc.sync.dma_start(out=out[rows, cols], in_=total[:, cols])

@@ -17,6 +17,7 @@ FP8X4 = mybir.dt.float8_e4m3fn_x4
 FP4X4 = mybir.dt.float4_e2m1fn_x4
 COPY = mybir.ActivationFunctionType.Copy
 RELU = mybir.ActivationFunctionType.Relu
+MAX = mybir.AluOpType.max
 MULT = mybir.AluOpType.mult
 ADD = mybir.AluOpType.add
 
@@ -27,6 +28,7 @@ CHUNKS = SLOTS // P
 K_TILES = K // P
 PER_COL = 16
 WINDOW = 768
+OWN, PARTNER = 0, 1
 
 
 def tile_moe_dub_relu2_kernel(
@@ -35,9 +37,7 @@ def tile_moe_dub_relu2_kernel(
     nc = tc.nc
     with ExitStack() as ctx:
         keep = ctx.enter_context(tc.tile_pool(name="keep", bufs=1))
-        sums_psum = ctx.enter_context(tc.psum_pool(name="sums_psum", bufs=2))
-        turned_psum = ctx.enter_context(tc.psum_pool(name="turned_psum", bufs=2))
-        grad_psum = ctx.enter_context(tc.psum_pool(name="grad_psum", bufs=4))
+        psum = ctx.enter_context(tc.psum_pool(name="psum", bufs=1))
 
         own_list = keep.tile([P, SLOTS // PER_COL], U16, name="own_list")
         partner_list = keep.tile([P, SLOTS // PER_COL], U16, name="partner_list")
@@ -51,6 +51,7 @@ def tile_moe_dub_relu2_kernel(
         wp_bytes = keep.tile([P, E, K], U8, name="wp_bytes", align_bytes=64)
         saved = [keep.tile([P, PACK, C], F32, name=f"saved{e}", align_bytes=64) for e in range(E)]
         gate_col = keep.tile([P, CHUNKS], F32, name="gate_col")
+        gate_twice = keep.tile([P, CHUNKS], F32, name="gate_twice")
         ones_diagonal = keep.tile([P, P], F32, name="ones_diagonal", align_bytes=64)
         identity = keep.tile([P, P], F32, name="identity", align_bytes=64)
 
@@ -78,14 +79,15 @@ def tile_moe_dub_relu2_kernel(
         nc.sync.dma_start(out=dy_codes[1][:], in_=dy_words[1].rearrange("p t d -> p (t d)").bitcast(I32))
         load_planes(nc.scalar, dy_bytes, dy_scales)
         load_w2(0)
-        load_planes(nc.scalar, w2_bytes, w2t_scales.rearrange("e s b i -> (e s) b i"))
+        load_planes(nc.sync, w2_bytes, w2t_scales.rearrange("e s b i -> (e s) b i"))
         with nc.allow_non_contiguous_dma(reason="one gate value a partition and chunk"):
             nc.sync.dma_start(out=gate_col[:], in_=gate[0:1, :].rearrange("o (c p) -> p (o c)", p=P))
         load_saved(0)
-        load_w2(1)
-        load_saved(1)
-        load_planes(nc.sync, w1_bytes, w1t_scales.rearrange("e s b k -> (e s) b k"))
         nc.sync.dma_start(out=w1_codes[:], in_=w1t_words.rearrange("e s p k d -> p (e s) (k d)").bitcast(I32))
+        load_w2(1)
+        load_planes(nc.sync, w1_bytes, w1t_scales.rearrange("e s b k -> (e s) b k"))
+        load_saved(1)
+        nc.sync.dma_start(out=wp_codes[:].bitcast(I32), in_=wpt_words.rearrange("e s p b -> p (e s) b").bitcast(I32))
         nc.sync.dma_start(partner_list[:], offs2)
         wp_rows = wpt_scales.rearrange("e s b k -> b (e s) k")
         for q in range(4):
@@ -93,8 +95,8 @@ def tile_moe_dub_relu2_kernel(
                 out=wp_bytes[32 * q : 32 * q + 4, :, :].bitcast(I32),
                 in_=wp_rows[4 * q : 4 * q + 4, :, :].bitcast(I32),
             )
-        nc.sync.dma_start(out=wp_codes[:].bitcast(I32), in_=wpt_words.rearrange("e s p b -> p (e s) b").bitcast(I32))
         nc.scalar.activation(out=identity[:], in_=ones_diagonal[:], func=RELU)
+        nc.scalar.mul(gate_twice[:], gate_col[:], 2.0)
 
         def list_cols(first, count):
             return slice(first // PER_COL, (first + count) // PER_COL)
@@ -112,17 +114,13 @@ def tile_moe_dub_relu2_kernel(
         dh_codes = [keep.tile([P, C], U32, name=f"dh_codes{e}", align_bytes=64) for e in range(E)]
         dh_bytes = [keep.tile([P, C], U8, name=f"dh_bytes{e}", align_bytes=64) for e in range(E)]
 
-        def hidden_gradient(c):
+        def bank(number, shape):
+            return psum.tile(shape, F32, name=f"bank{number}")
+
+        def hidden_gradient(c, sums_bank, turned_bank):
             e, half = divmod(c, C // P)
             cols = slice(half * P, (half + 1) * P)
-            slope = keep.tile([P, P * PACK], F32, name=f"slope{c}", align_bytes=64)
-            nc.scalar.activation(
-                out=slope[:].rearrange("p (u v t) -> p u t v", v=2, t=PACK),
-                in_=saved[e][:, :, cols].rearrange("p t (u v) -> p u t v", v=2),
-                func=RELU,
-                scale=2.0,
-            )
-            sums = sums_psum.tile([P, H], F32, name="sums")
+            sums = bank(sums_bank, [P, H])
             for s in range(PASSES):
                 nc.tensor.matmul_mx(
                     out=sums[:],
@@ -135,93 +133,116 @@ def tile_moe_dub_relu2_kernel(
                 )
             gated = keep.tile([P, PACK, P], F32, name=f"gated{c}", align_bytes=64)
             nc.scalar.activation(
-                out=gated[:], in_=sums[:].rearrange("j (m t) -> j t m", t=PACK), func=COPY, scale=gate_col[:, c : c + 1]
+                out=gated[:], in_=sums[:].rearrange("j (m t) -> j t m", t=PACK), func=COPY, scale=gate_twice[:, c : c + 1]
             )
-            turned = turned_psum.tile([P, PACK, P], F32, name="turned")
+            turned = bank(turned_bank, [P, PACK, P])
             for t in range(PACK):
                 nc.tensor.transpose(turned[:, t, :], gated[:, t, :], identity[:])
-            nc.vector.tensor_tensor(
-                out=dh[e][:, half * P * PACK : (half + 1) * P * PACK].rearrange("p (j t) -> p j t", t=PACK),
-                in0=turned[:].rearrange("p t j -> p j t"),
-                in1=slope[:].rearrange("p (j t) -> p j t", t=PACK),
-                op=MULT,
+            rounded = dh[e][:, half * P * PACK : (half + 1) * P * PACK].rearrange("p (j t) -> p j t", t=PACK)
+            nc.vector.scalar_tensor_tensor(
+                out=rounded,
+                in0=saved[e][:, :, cols].rearrange("p t j -> p j t"),
+                scalar=0.0,
+                in1=turned[:].rearrange("p t j -> p j t"),
+                op0=MAX,
+                op1=MULT,
             )
 
-        def quantise(e):
-            nc.vector.quantize_mx(out=dh_codes[e][:].bitcast(FP8X4), scales=dh_bytes[e][:], in_=dh[e][:])
+        def quantise(first, count):
+            e, place = divmod(first, C)
+            cols = slice(place, place + count)
+            nc.vector.quantize_mx(
+                out=dh_codes[e][:, cols].bitcast(FP8X4),
+                scales=dh_bytes[e][:, cols],
+                in_=dh[e][:, PACK * place : PACK * (place + count)],
+            )
 
         by_slot = [keep.tile([P, 2, SLOTS], F32, name=f"by_slot{kt}", align_bytes=64) for kt in range(K_TILES)]
+        by_token = [[keep.tile([P, WINDOW], F32, name=f"by_token{kt}{m}", align_bytes=64) for m in range(2)] for kt in range(K_TILES)]
+        lists = (own_list, partner_list)
 
-        def token_gradients(kt, e, apart):
+        def product(into, kt, m, first, count):
+            e, place = divmod(first, C)
             rows = slice(kt * P, (kt + 1) * P)
-            slots = slice(e * C, (e + 1) * C)
-            grads = grad_psum.tile([P, 2, C], F32, name="grads")
-            nc.tensor.matmul_mx(
-                out=grads[:, 0, :],
-                lhsT=w1_codes[:, e, rows].bitcast(FP8X4),
-                lhsT_scale=w1_bytes[4 * e :, rows],
-                rhs=dh_codes[e][:].bitcast(FP8X4),
-                rhs_scale=dh_bytes[e][:],
-                start=True,
-                stop=True,
-            )
-            if apart:
-                nc.scalar.copy(out=by_slot[kt][:, 0, slots], in_=grads[:, 0, :])
-                grads = grad_psum.tile([P, 2, C], F32, name="grads")
-            nc.tensor.matmul_mx(
-                out=grads[:, 1, :],
-                lhsT=wp_codes[:, e, 2 * kt * P : 2 * (kt + 1) * P].bitcast(FP4X4),
-                lhsT_scale=wp_bytes[:, e, rows],
-                rhs=dh_codes[e][:].bitcast(FP8X4),
-                rhs_scale=dh_bytes[e][:],
-                start=True,
-                stop=True,
-            )
-            if apart:
-                nc.scalar.copy(out=by_slot[kt][:, 1, slots], in_=grads[:, 1, :])
+            if m == OWN:
+                codes, scales = w1_codes[:, e, rows].bitcast(FP8X4), w1_bytes[4 * e :, rows]
             else:
-                nc.scalar.copy(out=by_slot[kt][:, :, slots], in_=grads[:])
+                codes, scales = wp_codes[:, e, 2 * kt * P : 2 * (kt + 1) * P].bitcast(FP4X4), wp_bytes[:, e, rows]
+            nc.tensor.matmul_mx(
+                out=into,
+                lhsT=codes,
+                lhsT_scale=scales,
+                rhs=dh_codes[e][:, place : place + count].bitcast(FP8X4),
+                rhs_scale=dh_bytes[e][:, place : place + count],
+                start=True,
+                stop=True,
+            )
 
-        hidden_gradient(0)
-        hidden_gradient(1)
-        quantise(0)
-        token_gradients(0, 0, True)
-        hidden_gradient(2)
-        hidden_gradient(3)
-        quantise(1)
-        token_gradients(0, 1, False)
-        for kt in range(1, K_TILES):
-            for e in range(E):
-                token_gradients(kt, e, False)
+        def pieces(number, wanted):
+            grads = bank(number, [P, 2, C])
+            for place, (kt, m, first, count) in enumerate(wanted):
+                product(grads[:, place, :count], kt, m, first, count)
+            for place, (kt, m, first, count) in enumerate(wanted):
+                nc.scalar.copy(out=by_slot[kt][:, m, first : first + count], in_=grads[:, place, :count])
 
-        for kt in range(K_TILES):
-            own = keep.tile([P, WINDOW], F32, name=f"own{kt}", align_bytes=64)
-            partner = keep.tile([P, WINDOW], F32, name=f"partner{kt}", align_bytes=64)
-            pieces = [(e * C, C) for e in range(E)] if kt == 0 else [(0, SLOTS)]
-            for first, count in pieces:
-                for m, (window, offsets) in enumerate(((own, own_list), (partner, partner_list))):
-                    nc.vector.tensor_copy(
-                        window[:].indirect(offsets[:, list_cols(first, count)]), by_slot[kt][:, m, first : first + count]
+        def scatter(kt, m, first, count):
+            nc.vector.tensor_copy(
+                by_token[kt][m][:].indirect(lists[m][:, list_cols(first, count)]), by_slot[kt][:, m, first : first + count]
+            )
+
+        def add_on_tensor(kt):
+            summed = bank(7, [P, T // P, P])
+            for b in range(T // P):
+                for m in range(2):
+                    nc.tensor.matmul(
+                        summed[:, b, :], by_token[kt][m][:, b * P : (b + 1) * P], identity[:],
+                        start=(m == 0), stop=(m == 1), is_transpose=True,
                     )
+            tokens_first = keep.tile([P, T // P, P], F32, name=f"tokens_first{kt}", align_bytes=64)
+            nc.scalar.copy(out=tokens_first[:], in_=summed[:])
+            back = bank(0, [P, T // P, P])
+            for b in range(T // P):
+                nc.tensor.transpose(back[:, b, :], tokens_first[:, b, :], identity[:])
             total = keep.tile([P, T], F32, name=f"total{kt}", align_bytes=64)
-            rows = slice(kt * P, (kt + 1) * P)
-            if kt < K_TILES - 1:
-                summed = turned_psum.tile([P, PACK, P], F32, name="turned")
-                for b in range(T // P):
-                    for m, window in enumerate((own, partner)):
-                        nc.tensor.matmul(
-                            summed[:, b, :], window[:, b * P : (b + 1) * P], identity[:],
-                            start=(m == 0), stop=(m == 1), is_transpose=True,
-                        )
-                by_token = keep.tile([P, T // P, P], F32, name=f"by_token{kt}", align_bytes=64)
-                nc.scalar.copy(out=by_token[:], in_=summed[:])
-                back = turned_psum.tile([P, PACK, P], F32, name="turned")
-                for b in range(T // P):
-                    nc.tensor.transpose(back[:, b, :], by_token[:, b, :], identity[:])
-                nc.scalar.copy(out=total[:], in_=back[:].rearrange("p b t -> p (b t)"))
-                nc.scalar.dma_start(out=out[rows, :], in_=total[:])
-            else:
-                for half in range(2):
-                    cols = slice(half * T // 2, (half + 1) * T // 2)
-                    nc.vector.tensor_tensor(total[:, cols], own[:, cols], partner[:, cols], ADD)
-                    nc.sync.dma_start(out=out[rows, cols], in_=total[:, cols])
+            nc.scalar.copy(out=total[:], in_=back[:].rearrange("p b t -> p (b t)"))
+            nc.scalar.dma_start(out=out[kt * P : (kt + 1) * P, :], in_=total[:])
+
+        def add_on_vector(kt):
+            total = keep.tile([P, T], F32, name=f"total{kt}", align_bytes=64)
+            for half in range(2):
+                cols = slice(half * T // 2, (half + 1) * T // 2)
+                nc.vector.tensor_tensor(total[:, cols], by_token[kt][OWN][:, cols], by_token[kt][PARTNER][:, cols], ADD)
+                nc.sync.dma_start(out=out[kt * P : (kt + 1) * P, cols], in_=total[:, cols])
+
+        hidden_gradient(0, 0, 2)
+        quantise(0, P)
+        hidden_gradient(1, 1, 3)
+        pieces(4, [(0, OWN, 0, P)])
+        quantise(P, P)
+        scatter(0, OWN, 0, P)
+        pieces(5, [(0, OWN, P, P)])
+        scatter(0, OWN, P, P)
+        pieces(6, [(1, OWN, 0, C), (2, OWN, 0, C)])
+        scatter(1, OWN, 0, C)
+        scatter(2, OWN, 0, C)
+        hidden_gradient(2, 5, 0)
+        hidden_gradient(3, 6, 1)
+        quantise(C, C)
+        pieces(0, [(0, PARTNER, 0, C), (1, PARTNER, 0, C)])
+        scatter(0, PARTNER, 0, C)
+        scatter(1, PARTNER, 0, C)
+        for kt in range(3):
+            pieces(2 + kt, [(kt, OWN, C, C), (kt, PARTNER, C, C)])
+        pieces(1, [(2, PARTNER, 0, C), (3, PARTNER, 0, C)])
+        pieces(5, [(3, OWN, 0, C), (3, OWN, C, C)])
+        pieces(6, [(3, PARTNER, C, C)])
+        for kt in (0, 1):
+            scatter(kt, OWN, C, C)
+            scatter(kt, PARTNER, C, C)
+            add_on_tensor(kt)
+        scatter(2, OWN, C, C)
+        scatter(2, PARTNER, 0, SLOTS)
+        add_on_tensor(2)
+        scatter(3, OWN, 0, SLOTS)
+        scatter(3, PARTNER, 0, SLOTS)
+        add_on_vector(3)

@@ -68,25 +68,30 @@ def tile_moe_dub_relu2_kernel(
                     in_=rows[:, 4 * q : 4 * q + 4, :].bitcast(I32),
                 )
 
-        def load_w2(e):
-            nc.sync.dma_start(out=w2_codes[e][:], in_=w2t_words[e].rearrange("s p i d -> p s (i d)").bitcast(I32))
+        def load_w2(e, passes):
+            words = w2t_words[e].rearrange("s p i d -> p s (i d)").bitcast(I32)
+            nc.sync.dma_start(out=w2_codes[e][:, passes, :], in_=words[:, passes, :])
 
         def load_saved(e):
             nc.sync.dma_start(out=saved[e][:], in_=a[:, e * C : (e + 1) * C].rearrange("(p t) j -> p t j", t=PACK))
 
-        nc.sync.dma_start(out=dy_codes[0][:], in_=dy_words[0].rearrange("p t d -> p (t d)").bitcast(I32))
+        def load_dy(s):
+            nc.sync.dma_start(out=dy_codes[s][:], in_=dy_words[s].rearrange("p t d -> p (t d)").bitcast(I32))
+
         nc.sync.dma_start(own_list[:], offs)
-        nc.sync.dma_start(out=dy_codes[1][:], in_=dy_words[1].rearrange("p t d -> p (t d)").bitcast(I32))
-        load_planes(nc.scalar, dy_bytes, dy_scales)
-        load_w2(0)
+        load_planes(nc.sync, dy_bytes, dy_scales)
+        load_dy(0)
+        load_w2(0, slice(0, 1))
+        load_dy(1)
         load_planes(nc.sync, w2_bytes, w2t_scales.rearrange("e s b i -> (e s) b i"))
+        load_w2(0, slice(1, 2))
         with nc.allow_non_contiguous_dma(reason="one gate value a partition and chunk"):
             nc.sync.dma_start(out=gate_col[:], in_=gate[0:1, :].rearrange("o (c p) -> p (o c)", p=P))
         load_saved(0)
-        nc.sync.dma_start(out=w1_codes[:], in_=w1t_words.rearrange("e s p k d -> p (e s) (k d)").bitcast(I32))
-        load_w2(1)
-        load_planes(nc.sync, w1_bytes, w1t_scales.rearrange("e s b k -> (e s) b k"))
+        load_w2(1, slice(0, PASSES))
         load_saved(1)
+        load_planes(nc.sync, w1_bytes, w1t_scales.rearrange("e s b k -> (e s) b k"))
+        nc.sync.dma_start(out=w1_codes[:], in_=w1t_words.rearrange("e s p k d -> p (e s) (k d)").bitcast(I32))
         nc.sync.dma_start(out=wp_codes[:].bitcast(I32), in_=wpt_words.rearrange("e s p b -> p (e s) b").bitcast(I32))
         nc.sync.dma_start(partner_list[:], offs2)
         wp_rows = wpt_scales.rearrange("e s b k -> b (e s) k")
@@ -178,12 +183,12 @@ def tile_moe_dub_relu2_kernel(
                 stop=True,
             )
 
-        def pieces(number, wanted):
-            grads = bank(number, [P, 2, C])
-            for place, (kt, m, first, count) in enumerate(wanted):
-                product(grads[:, place, :count], kt, m, first, count)
-            for place, (kt, m, first, count) in enumerate(wanted):
-                nc.scalar.copy(out=by_slot[kt][:, m, first : first + count], in_=grads[:, place, :count])
+        def products(number, kt, m, experts):
+            grads = bank(number, [P, E, C])
+            for e in experts:
+                product(grads[:, e, :], kt, m, e * C, C)
+            first, last = min(experts), max(experts) + 1
+            nc.scalar.copy(out=by_slot[kt][:, m, first * C : last * C], in_=grads[:, first:last, :].rearrange("p e c -> p (e c)"))
 
         def scatter(kt, m, first, count):
             nc.vector.tensor_copy(
@@ -215,32 +220,27 @@ def tile_moe_dub_relu2_kernel(
                 nc.sync.dma_start(out=out[kt * P : (kt + 1) * P, cols], in_=total[:, cols])
 
         hidden_gradient(0, 0, 2)
-        quantise(0, P)
         hidden_gradient(1, 1, 3)
-        pieces(4, [(0, OWN, 0, P)])
-        quantise(P, P)
-        scatter(0, OWN, 0, P)
-        pieces(5, [(0, OWN, P, P)])
-        scatter(0, OWN, P, P)
-        pieces(6, [(1, OWN, 0, C), (2, OWN, 0, C)])
-        scatter(1, OWN, 0, C)
-        scatter(2, OWN, 0, C)
-        hidden_gradient(2, 5, 0)
-        hidden_gradient(3, 6, 1)
+        quantise(0, C)
+        products(4, 0, OWN, [0])
+        hidden_gradient(2, 1, 0)
+        hidden_gradient(3, 2, 3)
         quantise(C, C)
-        pieces(0, [(0, PARTNER, 0, C), (1, PARTNER, 0, C)])
-        scatter(0, PARTNER, 0, C)
-        scatter(1, PARTNER, 0, C)
-        for kt in range(3):
-            pieces(2 + kt, [(kt, OWN, C, C), (kt, PARTNER, C, C)])
-        pieces(1, [(2, PARTNER, 0, C), (3, PARTNER, 0, C)])
-        pieces(5, [(3, OWN, 0, C), (3, OWN, C, C)])
-        pieces(6, [(3, PARTNER, C, C)])
-        for kt in (0, 1):
-            scatter(kt, OWN, C, C)
-            scatter(kt, PARTNER, C, C)
-            add_on_tensor(kt)
-        scatter(2, OWN, C, C)
+        products(5, 0, OWN, [1])
+        products(6, 1, OWN, [1, 0])
+        products(5, 0, PARTNER, [0, 1])
+        products(6, 1, PARTNER, [0, 1])
+        for kt in range(2, K_TILES):
+            products(5, kt, OWN, [0, 1])
+            products(6, kt, PARTNER, [0, 1])
+        scatter(0, OWN, 0, C)
+        scatter(0, OWN, C, C)
+        scatter(1, OWN, 0, SLOTS)
+        scatter(0, PARTNER, 0, SLOTS)
+        add_on_tensor(0)
+        scatter(1, PARTNER, 0, SLOTS)
+        add_on_tensor(1)
+        scatter(2, OWN, 0, SLOTS)
         scatter(2, PARTNER, 0, SLOTS)
         add_on_tensor(2)
         scatter(3, OWN, 0, SLOTS)

@@ -41,24 +41,25 @@ def tile_moe_dub_relu2_kernel(
 
         own_list = keep.tile([P, SLOTS // PER_COL], U16, name="own_list")
         partner_list = keep.tile([P, SLOTS // PER_COL], U16, name="partner_list")
-        dy_codes = [keep.tile([P, T], I32, name=f"dy_codes{s}", align_bytes=64) for s in range(PASSES)]
+        dy_codes = keep.tile([P, PASSES, T], I32, name="dy_codes", align_bytes=64)
         dy_bytes = keep.tile([P, T], U8, name="dy_bytes", align_bytes=64)
         w2_codes = [keep.tile([P, PASSES, H], I32, name=f"w2_codes{e}", align_bytes=64) for e in range(E)]
         w2_bytes = keep.tile([P, H], U8, name="w2_bytes", align_bytes=64)
-        w1_codes = keep.tile([P, E, K], I32, name="w1_codes", align_bytes=64)
+        w1_codes = [keep.tile([P, K], I32, name=f"w1_codes{e}", align_bytes=64) for e in range(E)]
         w1_bytes = keep.tile([P, K], U8, name="w1_bytes", align_bytes=64)
         wp_codes = keep.tile([P, E, 2 * K], U8, name="wp_codes", align_bytes=64)
         wp_bytes = keep.tile([P, E, K], U8, name="wp_bytes", align_bytes=64)
         saved = [keep.tile([P, PACK, C], F32, name=f"saved{e}", align_bytes=64) for e in range(E)]
-        gate_col = keep.tile([P, CHUNKS], F32, name="gate_col")
+        gate_rows = keep.tile([P, P], F32, name="gate_rows", align_bytes=64)
         gate_twice = keep.tile([P, CHUNKS], F32, name="gate_twice")
-        ones_diagonal = keep.tile([P, P], F32, name="ones_diagonal", align_bytes=64)
         identity = keep.tile([P, P], F32, name="identity", align_bytes=64)
 
-        for plane in (dy_bytes, w2_bytes, w1_bytes):
+        make_identity(nc, identity[:])
+        nc.vector.memset(dy_bytes[:].bitcast(I32), 0)
+        nc.vector.memset(gate_rows[:], 0.0)
+        for plane in (w2_bytes, w1_bytes):
             nc.vector.memset(plane[:].bitcast(I32), 0)
         nc.vector.memset(wp_bytes[:].rearrange("p e k -> p (e k)").bitcast(I32), 0)
-        make_identity(nc, ones_diagonal[:])
 
         def load_planes(queue, plane, rows):
             count = rows.shape[0]
@@ -68,30 +69,24 @@ def tile_moe_dub_relu2_kernel(
                     in_=rows[:, 4 * q : 4 * q + 4, :].bitcast(I32),
                 )
 
-        def load_w2(e, passes):
-            words = w2t_words[e].rearrange("s p i d -> p s (i d)").bitcast(I32)
-            nc.sync.dma_start(out=w2_codes[e][:, passes, :], in_=words[:, passes, :])
+        def load_w2(e):
+            nc.sync.dma_start(out=w2_codes[e][:], in_=w2t_words[e].rearrange("s p i d -> p s (i d)").bitcast(I32))
+
+        def load_w1(e):
+            nc.sync.dma_start(out=w1_codes[e][:], in_=w1t_words[e, 0].rearrange("p k d -> p (k d)").bitcast(I32))
 
         def load_saved(e):
             nc.sync.dma_start(out=saved[e][:], in_=a[:, e * C : (e + 1) * C].rearrange("(p t) j -> p t j", t=PACK))
 
-        def load_dy(s):
-            nc.sync.dma_start(out=dy_codes[s][:], in_=dy_words[s].rearrange("p t d -> p (t d)").bitcast(I32))
-
         nc.sync.dma_start(own_list[:], offs)
         load_planes(nc.sync, dy_bytes, dy_scales)
-        load_dy(0)
-        load_w2(0, slice(0, 1))
-        load_dy(1)
+        nc.sync.dma_start(out=gate_rows[0:CHUNKS, :], in_=gate[0:1, :].rearrange("o (c j) -> (o c) j", j=P))
+        nc.sync.dma_start(out=dy_codes[:], in_=dy_words.rearrange("s p t d -> p s (t d)").bitcast(I32))
+        load_w2(0)
         load_planes(nc.sync, w2_bytes, w2t_scales.rearrange("e s b i -> (e s) b i"))
-        load_w2(0, slice(1, 2))
-        with nc.allow_non_contiguous_dma(reason="one gate value a partition and chunk"):
-            nc.sync.dma_start(out=gate_col[:], in_=gate[0:1, :].rearrange("o (c p) -> p (o c)", p=P))
         load_saved(0)
-        load_w2(1, slice(0, PASSES))
-        load_saved(1)
+        load_w1(0)
         load_planes(nc.sync, w1_bytes, w1t_scales.rearrange("e s b k -> (e s) b k"))
-        nc.sync.dma_start(out=w1_codes[:], in_=w1t_words.rearrange("e s p k d -> p (e s) (k d)").bitcast(I32))
         nc.sync.dma_start(out=wp_codes[:].bitcast(I32), in_=wpt_words.rearrange("e s p b -> p (e s) b").bitcast(I32))
         nc.sync.dma_start(partner_list[:], offs2)
         wp_rows = wpt_scales.rearrange("e s b k -> b (e s) k")
@@ -100,8 +95,16 @@ def tile_moe_dub_relu2_kernel(
                 out=wp_bytes[32 * q : 32 * q + 4, :, :].bitcast(I32),
                 in_=wp_rows[4 * q : 4 * q + 4, :, :].bitcast(I32),
             )
-        nc.scalar.activation(out=identity[:], in_=ones_diagonal[:], func=RELU)
-        nc.scalar.mul(gate_twice[:], gate_col[:], 2.0)
+        load_w2(1)
+        load_saved(1)
+        load_w1(1)
+
+        def bank(number, shape):
+            return psum.tile(shape, F32, name=f"bank{number}")
+
+        gate_cols = bank("01", [P, P])
+        nc.tensor.transpose(gate_cols[:], gate_rows[:], identity[:])
+        nc.scalar.mul(gate_twice[:], gate_cols[:, 0:CHUNKS], 2.0)
 
         def list_cols(first, count):
             return slice(first // PER_COL, (first + count) // PER_COL)
@@ -112,45 +115,71 @@ def tile_moe_dub_relu2_kernel(
             e, place = divmod(first, C)
             picks = own_list[:, list_cols(first, count)]
             for s in range(PASSES):
-                nc.vector.tensor_copy(g_codes[e][s][:, place : place + count], dy_codes[s][:].bitcast(U32).indirect(picks))
+                nc.vector.tensor_copy(g_codes[e][s][:, place : place + count], dy_codes[:, s, :].bitcast(U32).indirect(picks))
             nc.vector.tensor_copy(g_bytes[e][:, place : place + count], dy_bytes[:].indirect(picks))
 
         dh = [keep.tile([P, C * PACK], BF16, name=f"dh{e}", align_bytes=64) for e in range(E)]
         dh_codes = [keep.tile([P, C], U32, name=f"dh_codes{e}", align_bytes=64) for e in range(E)]
         dh_bytes = [keep.tile([P, C], U8, name=f"dh_bytes{e}", align_bytes=64) for e in range(E)]
 
-        def bank(number, shape):
-            return psum.tile(shape, F32, name=f"bank{number}")
-
-        def hidden_gradient(c, sums_bank, turned_bank):
+        def hidden_gradient(c, sums_bank, parts, turned_bank):
             e, half = divmod(c, C // P)
             cols = slice(half * P, (half + 1) * P)
-            sums = bank(sums_bank, [P, H])
-            for s in range(PASSES):
-                nc.tensor.matmul_mx(
-                    out=sums[:],
-                    lhsT=g_codes[e][s][:, cols].bitcast(FP8X4),
-                    lhsT_scale=g_bytes[e][4 * s :, cols],
-                    rhs=w2_codes[e][:, s, :].bitcast(FP8X4),
-                    rhs_scale=w2_bytes[4 * (PASSES * e + s) :, :],
-                    start=(s == 0),
-                    stop=(s == PASSES - 1),
-                )
             gated = keep.tile([P, PACK, P], F32, name=f"gated{c}", align_bytes=64)
-            nc.scalar.activation(
-                out=gated[:], in_=sums[:].rearrange("j (m t) -> j t m", t=PACK), func=COPY, scale=gate_twice[:, c : c + 1]
-            )
+            width = H // parts
+            banks = bank(sums_bank, [P, parts, H])
+            for part in range(parts):
+                hidden = slice(part * width, (part + 1) * width)
+                sums = banks[:, part, 0:width]
+                for s in range(PASSES):
+                    nc.tensor.matmul_mx(
+                        out=sums,
+                        lhsT=g_codes[e][s][:, cols].bitcast(FP8X4),
+                        lhsT_scale=g_bytes[e][4 * s :, cols],
+                        rhs=w2_codes[e][:, s, hidden].bitcast(FP8X4),
+                        rhs_scale=w2_bytes[4 * (PASSES * e + s) :, hidden],
+                        start=(s == 0),
+                        stop=(s == PASSES - 1),
+                    )
+                nc.scalar.activation(
+                    out=gated[:, :, part * width // PACK : (part + 1) * width // PACK],
+                    in_=sums.rearrange("j (m t) -> j t m", t=PACK),
+                    func=COPY,
+                    scale=gate_twice[:, c : c + 1],
+                )
             turned = bank(turned_bank, [P, PACK, P])
             for t in range(PACK):
                 nc.tensor.transpose(turned[:, t, :], gated[:, t, :], identity[:])
-            rounded = dh[e][:, half * P * PACK : (half + 1) * P * PACK].rearrange("p (j t) -> p j t", t=PACK)
+            return turned
+
+        def rounded(c):
+            e, half = divmod(c, C // P)
+            return dh[e][:, half * P * PACK : (half + 1) * P * PACK]
+
+        def saved_by_slot(c):
+            e, half = divmod(c, C // P)
+            return saved[e][:, :, half * P : (half + 1) * P].rearrange("p t j -> p j t")
+
+        def mask_on_vector(c, turned):
             nc.vector.scalar_tensor_tensor(
-                out=rounded,
-                in0=saved[e][:, :, cols].rearrange("p t j -> p j t"),
+                out=rounded(c).rearrange("p (j t) -> p j t", t=PACK),
+                in0=saved_by_slot(c),
                 scalar=0.0,
                 in1=turned[:].rearrange("p t j -> p j t"),
                 op0=MAX,
                 op1=MULT,
+            )
+
+        def positive_part(c, place):
+            positive = keep.tile([P, P, PACK], F32, name=place, align_bytes=64)
+            nc.scalar.activation(out=positive[:], in_=saved_by_slot(c), func=RELU)
+            return positive
+
+        def mask_on_gpsimd(c, turned, positive, place):
+            woven = keep.tile([P, P, PACK], F32, name=place, align_bytes=64)
+            nc.scalar.copy(out=woven[:], in_=turned[:].rearrange("p t j -> p j t"))
+            nc.gpsimd.tensor_tensor(
+                rounded(c), woven[:].rearrange("p j t -> p (j t)"), positive[:].rearrange("p j t -> p (j t)"), MULT
             )
 
         def quantise(first, count):
@@ -162,7 +191,7 @@ def tile_moe_dub_relu2_kernel(
                 in_=dh[e][:, PACK * place : PACK * (place + count)],
             )
 
-        by_slot = [keep.tile([P, 2, SLOTS], F32, name=f"by_slot{kt}", align_bytes=64) for kt in range(K_TILES)]
+        by_slot = {}
         by_token = [[keep.tile([P, WINDOW], F32, name=f"by_token{kt}{m}", align_bytes=64) for m in range(2)] for kt in range(K_TILES)]
         lists = (own_list, partner_list)
 
@@ -170,7 +199,7 @@ def tile_moe_dub_relu2_kernel(
             e, place = divmod(first, C)
             rows = slice(kt * P, (kt + 1) * P)
             if m == OWN:
-                codes, scales = w1_codes[:, e, rows].bitcast(FP8X4), w1_bytes[4 * e :, rows]
+                codes, scales = w1_codes[e][:, rows].bitcast(FP8X4), w1_bytes[4 * e :, rows]
             else:
                 codes, scales = wp_codes[:, e, 2 * kt * P : 2 * (kt + 1) * P].bitcast(FP4X4), wp_bytes[:, e, rows]
             nc.tensor.matmul_mx(
@@ -183,34 +212,24 @@ def tile_moe_dub_relu2_kernel(
                 stop=True,
             )
 
-        def products(number, kt, m, experts):
-            grads = bank(number, [P, E, C])
-            for e in experts:
-                product(grads[:, e, :], kt, m, e * C, C)
-            first, last = min(experts), max(experts) + 1
-            nc.scalar.copy(out=by_slot[kt][:, m, first * C : last * C], in_=grads[:, first:last, :].rearrange("p e c -> p (e c)"))
+        def products(number, kt, m, first, count, place=None):
+            grads = bank(number, [P, count])
+            piece = keep.tile([P, count], F32, name=place or f"by_slot{kt}{m}{first}", align_bytes=64)
+            by_slot[(kt, m, first)] = piece
+            width = min(count, C)
+            for col in range(0, count, width):
+                product(grads[:, col : col + width], kt, m, first + col, width)
+            nc.scalar.copy(out=piece[:], in_=grads[:])
 
         def scatter(kt, m, first, count):
             nc.vector.tensor_copy(
-                by_token[kt][m][:].indirect(lists[m][:, list_cols(first, count)]), by_slot[kt][:, m, first : first + count]
+                by_token[kt][m][:].indirect(lists[m][:, list_cols(first, count)]), by_slot[(kt, m, first)][:]
             )
 
-        def add_on_tensor(kt):
-            summed = bank(7, [P, T // P, P])
-            for b in range(T // P):
-                for m in range(2):
-                    nc.tensor.matmul(
-                        summed[:, b, :], by_token[kt][m][:, b * P : (b + 1) * P], identity[:],
-                        start=(m == 0), stop=(m == 1), is_transpose=True,
-                    )
-            tokens_first = keep.tile([P, T // P, P], F32, name=f"tokens_first{kt}", align_bytes=64)
-            nc.scalar.copy(out=tokens_first[:], in_=summed[:])
-            back = bank(0, [P, T // P, P])
-            for b in range(T // P):
-                nc.tensor.transpose(back[:, b, :], tokens_first[:, b, :], identity[:])
+        def add_on_gpsimd(kt):
             total = keep.tile([P, T], F32, name=f"total{kt}", align_bytes=64)
-            nc.scalar.copy(out=total[:], in_=back[:].rearrange("p b t -> p (b t)"))
-            nc.scalar.dma_start(out=out[kt * P : (kt + 1) * P, :], in_=total[:])
+            nc.gpsimd.tensor_tensor(total[:], by_token[kt][OWN][:, 0:T], by_token[kt][PARTNER][:, 0:T], ADD)
+            nc.sync.dma_start(out=out[kt * P : (kt + 1) * P, :], in_=total[:])
 
         def add_on_vector(kt):
             total = keep.tile([P, T], F32, name=f"total{kt}", align_bytes=64)
@@ -219,30 +238,40 @@ def tile_moe_dub_relu2_kernel(
                 nc.vector.tensor_tensor(total[:, cols], by_token[kt][OWN][:, cols], by_token[kt][PARTNER][:, cols], ADD)
                 nc.sync.dma_start(out=out[kt * P : (kt + 1) * P, cols], in_=total[:, cols])
 
-        hidden_gradient(0, 0, 2)
-        hidden_gradient(1, 1, 3)
-        quantise(0, C)
-        products(4, 0, OWN, [0])
-        hidden_gradient(2, 1, 0)
-        hidden_gradient(3, 2, 3)
+        turned0 = hidden_gradient(0, "01", 2, 2)
+        turned1 = hidden_gradient(1, 3, 1, 4)
+        mask_on_vector(0, turned0)
+        quantise(0, P)
+        products(5, 0, OWN, 0, P)
+        products(6, 1, OWN, 0, P)
+        mask_on_vector(1, turned1)
+        quantise(P, P)
+        products(7, 0, OWN, P, P, "late0")
+        products(5, 1, OWN, P, P, "late1")
+        products(6, 2, OWN, 0, C)
+        products(3, 3, OWN, 0, C)
+        for first in (0, P):
+            for kt in range(2):
+                scatter(kt, OWN, first, P)
+        scatter(2, OWN, 0, C)
+        scatter(3, OWN, 0, C)
+        turned2 = hidden_gradient(2, 7, 1, 2)
+        turned3 = hidden_gradient(3, 5, 1, 4)
+        for kt in range(K_TILES - 1):
+            products(6 - 3 * (kt % 2), kt, PARTNER, 0, C)
+            scatter(kt, PARTNER, 0, C)
+        mask_on_gpsimd(2, turned2, positive_part(2, "late0"), "woven2")
+        mask_on_gpsimd(3, turned3, positive_part(3, "late1"), "woven3")
         quantise(C, C)
-        products(5, 0, OWN, [1])
-        products(6, 1, OWN, [1, 0])
-        products(5, 0, PARTNER, [0, 1])
-        products(6, 1, PARTNER, [0, 1])
-        for kt in range(2, K_TILES):
-            products(5, kt, OWN, [0, 1])
-            products(6, kt, PARTNER, [0, 1])
-        scatter(0, OWN, 0, C)
-        scatter(0, OWN, C, C)
-        scatter(1, OWN, 0, SLOTS)
-        scatter(0, PARTNER, 0, SLOTS)
-        add_on_tensor(0)
-        scatter(1, PARTNER, 0, SLOTS)
-        add_on_tensor(1)
-        scatter(2, OWN, 0, SLOTS)
-        scatter(2, PARTNER, 0, SLOTS)
-        add_on_tensor(2)
-        scatter(3, OWN, 0, SLOTS)
-        scatter(3, PARTNER, 0, SLOTS)
-        add_on_vector(3)
+        products(3, 3, PARTNER, 0, C, "woven3")
+        scatter(3, PARTNER, 0, C)
+        for kt in range(K_TILES):
+            products(5 + kt % 2, kt, OWN, C, C)
+            products(7 - 5 * (kt % 2), kt, PARTNER, C, C)
+        for kt in range(K_TILES):
+            scatter(kt, OWN, C, C)
+            scatter(kt, PARTNER, C, C)
+            if kt < K_TILES - 1:
+                add_on_gpsimd(kt)
+            else:
+                add_on_vector(kt)

@@ -29,6 +29,7 @@ K_TILES = K // P
 PER_COL = 16
 WINDOW = 768
 OWN, PARTNER = 0, 1
+WARM_UPS = 4
 
 
 def tile_moe_dub_relu2_kernel(
@@ -102,9 +103,26 @@ def tile_moe_dub_relu2_kernel(
         def bank(number, shape):
             return psum.tile(shape, F32, name=f"bank{number}")
 
-        gate_cols = bank("01", [P, P])
+        gate_cols = bank(7, [P, P])
         nc.tensor.transpose(gate_cols[:], gate_rows[:], identity[:])
         nc.scalar.mul(gate_twice[:], gate_cols[:, 0:CHUNKS], 2.0)
+
+        ones = keep.tile([P, PACK * H], BF16, name="ones", align_bytes=64)
+        warm_codes = keep.tile([P, H], U32, name="warm_codes", align_bytes=64)
+        warm_bytes = keep.tile([P, H], U8, name="warm_bytes", align_bytes=64)
+        nc.vector.memset(ones[:].bitcast(I32), 0x3F803F80)
+        nc.vector.quantize_mx(out=warm_codes[:].bitcast(FP8X4), scales=warm_bytes[:], in_=ones[:])
+        warm = bank(6, [P, H])
+        for n in range(WARM_UPS):
+            nc.tensor.matmul_mx(
+                out=warm[:],
+                lhsT=warm_codes[:, 0:P].bitcast(FP8X4),
+                lhsT_scale=warm_bytes[:, 0:P],
+                rhs=warm_codes[:].bitcast(FP8X4),
+                rhs_scale=warm_bytes[:],
+                start=True,
+                stop=True,
+            )
 
         def list_cols(first, count):
             return slice(first // PER_COL, (first + count) // PER_COL)

@@ -27,9 +27,10 @@ PASSES = N // (P * PACK)
 CHUNKS = SLOTS // P
 K_TILES = K // P
 PER_COL = 16
-WINDOW = 768
+WINDOW = 512
 OWN, PARTNER = 0, 1
 WARM_UPS = 4
+HALF = P // 2
 
 
 def tile_moe_dub_relu2_kernel(
@@ -42,7 +43,7 @@ def tile_moe_dub_relu2_kernel(
 
         own_list = keep.tile([P, SLOTS // PER_COL], U16, name="own_list")
         partner_list = keep.tile([P, SLOTS // PER_COL], U16, name="partner_list")
-        dy_codes = keep.tile([P, PASSES, T], I32, name="dy_codes", align_bytes=64)
+        dy_codes = keep.tile([P, PASSES * T], I32, name="dy_codes", align_bytes=64)
         dy_bytes = keep.tile([P, T], U8, name="dy_bytes", align_bytes=64)
         w2_codes = [keep.tile([P, PASSES, H], I32, name=f"w2_codes{e}", align_bytes=64) for e in range(E)]
         w2_bytes = keep.tile([P, H], U8, name="w2_bytes", align_bytes=64)
@@ -51,13 +52,12 @@ def tile_moe_dub_relu2_kernel(
         wp_codes = keep.tile([P, E, 2 * K], U8, name="wp_codes", align_bytes=64)
         wp_bytes = keep.tile([P, E, K], U8, name="wp_bytes", align_bytes=64)
         saved = [keep.tile([P, PACK, C], F32, name=f"saved{e}", align_bytes=64) for e in range(E)]
-        gate_rows = keep.tile([P, P], F32, name="gate_rows", align_bytes=64)
+        gate_col = keep.tile([P, CHUNKS], F32, name="gate_col")
         gate_twice = keep.tile([P, CHUNKS], F32, name="gate_twice")
         identity = keep.tile([P, P], F32, name="identity", align_bytes=64)
 
         make_identity(nc, identity[:])
         nc.vector.memset(dy_bytes[:].bitcast(I32), 0)
-        nc.vector.memset(gate_rows[:], 0.0)
         for plane in (w2_bytes, w1_bytes):
             nc.vector.memset(plane[:].bitcast(I32), 0)
         nc.vector.memset(wp_bytes[:].rearrange("p e k -> p (e k)").bitcast(I32), 0)
@@ -73,6 +73,9 @@ def tile_moe_dub_relu2_kernel(
         def load_w2(e):
             nc.sync.dma_start(out=w2_codes[e][:], in_=w2t_words[e].rearrange("s p i d -> p s (i d)").bitcast(I32))
 
+        def load_dy(s):
+            nc.sync.dma_start(out=dy_codes[:, s * T : (s + 1) * T], in_=dy_words[s].rearrange("p t d -> p (t d)").bitcast(I32))
+
         def load_w1(e):
             nc.sync.dma_start(out=w1_codes[e][:], in_=w1t_words[e, 0].rearrange("p k d -> p (k d)").bitcast(I32))
 
@@ -80,11 +83,13 @@ def tile_moe_dub_relu2_kernel(
             nc.sync.dma_start(out=saved[e][:], in_=a[:, e * C : (e + 1) * C].rearrange("(p t) j -> p t j", t=PACK))
 
         nc.sync.dma_start(own_list[:], offs)
+        load_dy(0)
         load_planes(nc.sync, dy_bytes, dy_scales)
-        nc.sync.dma_start(out=gate_rows[0:CHUNKS, :], in_=gate[0:1, :].rearrange("o (c j) -> (o c) j", j=P))
-        nc.sync.dma_start(out=dy_codes[:], in_=dy_words.rearrange("s p t d -> p s (t d)").bitcast(I32))
+        load_dy(1)
         load_w2(0)
         load_planes(nc.sync, w2_bytes, w2t_scales.rearrange("e s b i -> (e s) b i"))
+        with nc.allow_non_contiguous_dma(reason="one gate value a partition and chunk"):
+            nc.sync.dma_start(out=gate_col[:], in_=gate[0:1, :].rearrange("o (c p) -> p (o c)", p=P))
         load_saved(0)
         load_w1(0)
         load_planes(nc.sync, w1_bytes, w1t_scales.rearrange("e s b k -> (e s) b k"))
@@ -103,9 +108,7 @@ def tile_moe_dub_relu2_kernel(
         def bank(number, shape):
             return psum.tile(shape, F32, name=f"bank{number}")
 
-        gate_cols = bank(7, [P, P])
-        nc.tensor.transpose(gate_cols[:], gate_rows[:], identity[:])
-        nc.scalar.mul(gate_twice[:], gate_cols[:, 0:CHUNKS], 2.0)
+        nc.scalar.mul(gate_twice[:], gate_col[:], 2.0)
 
         ones = keep.tile([P, PACK * H], BF16, name="ones", align_bytes=64)
         warm_codes = keep.tile([P, H], U32, name="warm_codes", align_bytes=64)
@@ -133,22 +136,23 @@ def tile_moe_dub_relu2_kernel(
             e, place = divmod(first, C)
             picks = own_list[:, list_cols(first, count)]
             for s in range(PASSES):
-                nc.vector.tensor_copy(g_codes[e][s][:, place : place + count], dy_codes[:, s, :].bitcast(U32).indirect(picks))
+                last = T if (first, s) == (0, 0) else PASSES * T
+                window = dy_codes[:, s * T : last].bitcast(U32)
+                nc.vector.tensor_copy(g_codes[e][s][:, place : place + count], window.indirect(picks))
             nc.vector.tensor_copy(g_bytes[e][:, place : place + count], dy_bytes[:].indirect(picks))
 
         dh = [keep.tile([P, C * PACK], BF16, name=f"dh{e}", align_bytes=64) for e in range(E)]
         dh_codes = [keep.tile([P, C], U32, name=f"dh_codes{e}", align_bytes=64) for e in range(E)]
         dh_bytes = [keep.tile([P, C], U8, name=f"dh_bytes{e}", align_bytes=64) for e in range(E)]
 
-        def hidden_gradient(c, sums_bank, parts, turned_bank):
+        def hidden_gradient(c, sums_banks, turned_bank):
             e, half = divmod(c, C // P)
             cols = slice(half * P, (half + 1) * P)
             gated = keep.tile([P, PACK, P], F32, name=f"gated{c}", align_bytes=64)
-            width = H // parts
-            banks = bank(sums_bank, [P, parts, H])
-            for part in range(parts):
+            width = H // len(sums_banks)
+            for part, number in enumerate(sums_banks):
                 hidden = slice(part * width, (part + 1) * width)
-                sums = banks[:, part, 0:width]
+                sums = bank(number, [P, width])[:]
                 for s in range(PASSES):
                     nc.tensor.matmul_mx(
                         out=sums,
@@ -178,12 +182,12 @@ def tile_moe_dub_relu2_kernel(
             e, half = divmod(c, C // P)
             return saved[e][:, :, half * P : (half + 1) * P].rearrange("p t j -> p j t")
 
-        def mask_on_vector(c, turned):
+        def mask_on_vector(c, turned, slots=slice(0, P)):
             nc.vector.scalar_tensor_tensor(
-                out=rounded(c).rearrange("p (j t) -> p j t", t=PACK),
-                in0=saved_by_slot(c),
+                out=rounded(c).rearrange("p (j t) -> p j t", t=PACK)[:, slots, :],
+                in0=saved_by_slot(c)[:, slots, :],
                 scalar=0.0,
-                in1=turned[:].rearrange("p t j -> p j t"),
+                in1=turned[:].rearrange("p t j -> p j t")[:, slots, :],
                 op0=MAX,
                 op1=MULT,
             )
@@ -256,25 +260,30 @@ def tile_moe_dub_relu2_kernel(
                 nc.vector.tensor_tensor(total[:, cols], by_token[kt][OWN][:, cols], by_token[kt][PARTNER][:, cols], ADD)
                 nc.sync.dma_start(out=out[kt * P : (kt + 1) * P, cols], in_=total[:, cols])
 
-        turned0 = hidden_gradient(0, "01", 2, 2)
-        turned1 = hidden_gradient(1, 3, 1, 4)
-        mask_on_vector(0, turned0)
-        quantise(0, P)
-        products(5, 0, OWN, 0, P)
+        turned0 = hidden_gradient(0, [0, 1], 2)
+        turned1 = hidden_gradient(1, [3], 4)
+        mask_on_vector(0, turned0, slice(0, HALF))
+        quantise(0, HALF)
+        products(5, 0, OWN, 0, HALF)
+        mask_on_vector(0, turned0, slice(HALF, P))
+        quantise(HALF, HALF)
         products(6, 1, OWN, 0, P)
+        products(0, 0, OWN, HALF, HALF)
         mask_on_vector(1, turned1)
         quantise(P, P)
-        products(7, 0, OWN, P, P, "late0")
         products(5, 1, OWN, P, P, "late1")
+        products(7, 0, OWN, P, P, "late0")
         products(6, 2, OWN, 0, C)
         products(3, 3, OWN, 0, C)
-        for first in (0, P):
-            for kt in range(2):
-                scatter(kt, OWN, first, P)
+        scatter(0, OWN, 0, HALF)
+        scatter(1, OWN, 0, P)
+        scatter(0, OWN, HALF, HALF)
+        scatter(1, OWN, P, P)
+        scatter(0, OWN, P, P)
         scatter(2, OWN, 0, C)
         scatter(3, OWN, 0, C)
-        turned2 = hidden_gradient(2, 7, 1, 2)
-        turned3 = hidden_gradient(3, 5, 1, 4)
+        turned2 = hidden_gradient(2, [7], 2)
+        turned3 = hidden_gradient(3, [5], 4)
         for kt in range(K_TILES - 1):
             products(6 - 3 * (kt % 2), kt, PARTNER, 0, C)
             scatter(kt, PARTNER, 0, C)

@@ -24,13 +24,13 @@ ADD = mybir.AluOpType.add
 P = 128
 PACK = 4
 PASSES = N // (P * PACK)
-CHUNKS = SLOTS // P
 K_TILES = K // P
+LAST = K_TILES - 1
 PER_COL = 16
-WINDOW = 512
+HALF = P // 2
 OWN, PARTNER = 0, 1
 WARM_UPS = 4
-HALF = P // 2
+TWO_ONES = 0x3F803F80
 
 
 def tile_moe_dub_relu2_kernel(
@@ -52,20 +52,25 @@ def tile_moe_dub_relu2_kernel(
         wp_codes = keep.tile([P, E, 2 * K], U8, name="wp_codes", align_bytes=64)
         wp_bytes = keep.tile([P, E, K], U8, name="wp_bytes", align_bytes=64)
         saved = [keep.tile([P, PACK, C], F32, name=f"saved{e}", align_bytes=64) for e in range(E)]
-        gate_col = keep.tile([P, CHUNKS], F32, name="gate_col")
-        gate_twice = keep.tile([P, CHUNKS], F32, name="gate_twice")
+        gate_col = [keep.tile([P, C // P], F32, name=f"gate_col{e}") for e in range(E)]
+        gate_twice = keep.tile([P, C // P], F32, name="gate_twice")
         identity = keep.tile([P, P], F32, name="identity", align_bytes=64)
 
         make_identity(nc, identity[:])
         nc.vector.memset(dy_bytes[:].bitcast(I32), 0)
-        for plane in (w2_bytes, w1_bytes):
-            nc.vector.memset(plane[:].bitcast(I32), 0)
+        nc.vector.memset(w2_bytes[:].bitcast(I32), 0)
+        ones = keep.tile([P, PACK * H], BF16, name="ones", align_bytes=64)
+        warm_codes = keep.tile([P, H], U32, name="warm_codes", align_bytes=64)
+        warm_bytes = keep.tile([P, H], U8, name="warm_bytes", align_bytes=64)
+        nc.vector.memset(ones[:].bitcast(I32), TWO_ONES)
+        nc.vector.quantize_mx(out=warm_codes[:].bitcast(FP8X4), scales=warm_bytes[:], in_=ones[:])
+        nc.vector.memset(w1_bytes[:].bitcast(I32), 0)
         nc.vector.memset(wp_bytes[:].rearrange("p e k -> p (e k)").bitcast(I32), 0)
 
-        def load_planes(queue, plane, rows):
+        def load_planes(plane, rows):
             count = rows.shape[0]
             for q in range(4):
-                queue.dma_start(
+                nc.sync.dma_start(
                     out=plane[32 * q : 32 * q + 4 * count, :].bitcast(I32),
                     in_=rows[:, 4 * q : 4 * q + 4, :].bitcast(I32),
                 )
@@ -76,6 +81,10 @@ def tile_moe_dub_relu2_kernel(
         def load_dy(s):
             nc.sync.dma_start(out=dy_codes[:, s * T : (s + 1) * T], in_=dy_words[s].rearrange("p t d -> p (t d)").bitcast(I32))
 
+        def load_gate(e):
+            with nc.allow_non_contiguous_dma(reason="one gate value a partition and chunk"):
+                nc.sync.dma_start(out=gate_col[e][:], in_=gate[0:1, e * C : (e + 1) * C].rearrange("o (c p) -> p (o c)", p=P))
+
         def load_w1(e):
             nc.sync.dma_start(out=w1_codes[e][:], in_=w1t_words[e, 0].rearrange("p k d -> p (k d)").bitcast(I32))
 
@@ -84,15 +93,14 @@ def tile_moe_dub_relu2_kernel(
 
         nc.sync.dma_start(own_list[:], offs)
         load_dy(0)
-        load_planes(nc.sync, dy_bytes, dy_scales)
+        load_planes(dy_bytes, dy_scales)
         load_dy(1)
         load_w2(0)
-        load_planes(nc.sync, w2_bytes, w2t_scales.rearrange("e s b i -> (e s) b i"))
-        with nc.allow_non_contiguous_dma(reason="one gate value a partition and chunk"):
-            nc.sync.dma_start(out=gate_col[:], in_=gate[0:1, :].rearrange("o (c p) -> p (o c)", p=P))
+        load_planes(w2_bytes, w2t_scales.rearrange("e s b i -> (e s) b i"))
+        load_gate(0)
         load_saved(0)
         load_w1(0)
-        load_planes(nc.sync, w1_bytes, w1t_scales.rearrange("e s b k -> (e s) b k"))
+        load_planes(w1_bytes, w1t_scales.rearrange("e s b k -> (e s) b k"))
         nc.sync.dma_start(out=wp_codes[:].bitcast(I32), in_=wpt_words.rearrange("e s p b -> p (e s) b").bitcast(I32))
         nc.sync.dma_start(partner_list[:], offs2)
         wp_rows = wpt_scales.rearrange("e s b k -> b (e s) k")
@@ -101,6 +109,7 @@ def tile_moe_dub_relu2_kernel(
                 out=wp_bytes[32 * q : 32 * q + 4, :, :].bitcast(I32),
                 in_=wp_rows[4 * q : 4 * q + 4, :, :].bitcast(I32),
             )
+        load_gate(1)
         load_w2(1)
         load_saved(1)
         load_w1(1)
@@ -108,13 +117,9 @@ def tile_moe_dub_relu2_kernel(
         def bank(number, shape):
             return psum.tile(shape, F32, name=f"bank{number}")
 
-        nc.scalar.mul(gate_twice[:], gate_col[:], 2.0)
+        nc.scalar.mul(gate_twice[:], gate_col[0][:], 2.0)
+        gate_scale = (gate_twice, gate_col[1])
 
-        ones = keep.tile([P, PACK * H], BF16, name="ones", align_bytes=64)
-        warm_codes = keep.tile([P, H], U32, name="warm_codes", align_bytes=64)
-        warm_bytes = keep.tile([P, H], U8, name="warm_bytes", align_bytes=64)
-        nc.vector.memset(ones[:].bitcast(I32), 0x3F803F80)
-        nc.vector.quantize_mx(out=warm_codes[:].bitcast(FP8X4), scales=warm_bytes[:], in_=ones[:])
         warm = bank(6, [P, H])
         for n in range(WARM_UPS):
             nc.tensor.matmul_mx(
@@ -136,8 +141,8 @@ def tile_moe_dub_relu2_kernel(
             e, place = divmod(first, C)
             picks = own_list[:, list_cols(first, count)]
             for s in range(PASSES):
-                last = T if (first, s) == (0, 0) else PASSES * T
-                window = dy_codes[:, s * T : last].bitcast(U32)
+                end = T if (first, s) == (0, 0) else PASSES * T
+                window = dy_codes[:, s * T : end].bitcast(U32)
                 nc.vector.tensor_copy(g_codes[e][s][:, place : place + count], window.indirect(picks))
             nc.vector.tensor_copy(g_bytes[e][:, place : place + count], dy_bytes[:].indirect(picks))
 
@@ -145,9 +150,9 @@ def tile_moe_dub_relu2_kernel(
         dh_codes = [keep.tile([P, C], U32, name=f"dh_codes{e}", align_bytes=64) for e in range(E)]
         dh_bytes = [keep.tile([P, C], U8, name=f"dh_bytes{e}", align_bytes=64) for e in range(E)]
 
-        def hidden_gradient(c, sums_banks, turned_bank):
-            e, half = divmod(c, C // P)
-            cols = slice(half * P, (half + 1) * P)
+        def gated_sums(c, sums_banks, turned_bank):
+            e, within = divmod(c, C // P)
+            cols = slice(within * P, (within + 1) * P)
             gated = keep.tile([P, PACK, P], F32, name=f"gated{c}", align_bytes=64)
             width = H // len(sums_banks)
             for part, number in enumerate(sums_banks):
@@ -167,7 +172,7 @@ def tile_moe_dub_relu2_kernel(
                     out=gated[:, :, part * width // PACK : (part + 1) * width // PACK],
                     in_=sums.rearrange("j (m t) -> j t m", t=PACK),
                     func=COPY,
-                    scale=gate_twice[:, c : c + 1],
+                    scale=gate_scale[e][:, within : within + 1],
                 )
             turned = bank(turned_bank, [P, PACK, P])
             for t in range(PACK):
@@ -175,14 +180,14 @@ def tile_moe_dub_relu2_kernel(
             return turned
 
         def rounded(c):
-            e, half = divmod(c, C // P)
-            return dh[e][:, half * P * PACK : (half + 1) * P * PACK]
+            e, within = divmod(c, C // P)
+            return dh[e][:, within * P * PACK : (within + 1) * P * PACK]
 
         def saved_by_slot(c):
-            e, half = divmod(c, C // P)
-            return saved[e][:, :, half * P : (half + 1) * P].rearrange("p t j -> p j t")
+            e, within = divmod(c, C // P)
+            return saved[e][:, :, within * P : (within + 1) * P].rearrange("p t j -> p j t")
 
-        def mask_on_vector(c, turned, slots=slice(0, P)):
+        def mask_on_vector(c, turned, slots):
             nc.vector.scalar_tensor_tensor(
                 out=rounded(c).rearrange("p (j t) -> p j t", t=PACK)[:, slots, :],
                 in0=saved_by_slot(c)[:, slots, :],
@@ -192,13 +197,13 @@ def tile_moe_dub_relu2_kernel(
                 op1=MULT,
             )
 
-        def positive_part(c, place):
-            positive = keep.tile([P, P, PACK], F32, name=place, align_bytes=64)
-            nc.scalar.activation(out=positive[:], in_=saved_by_slot(c), func=RELU)
+        def positive_part(c, tag):
+            positive = keep.tile([P, P, PACK], F32, name=tag, align_bytes=64)
+            nc.scalar.activation(out=positive[:], in_=saved_by_slot(c), func=RELU, scale=2.0)
             return positive
 
-        def mask_on_gpsimd(c, turned, positive, place):
-            woven = keep.tile([P, P, PACK], F32, name=place, align_bytes=64)
+        def mask_on_gpsimd(c, turned, positive, tag):
+            woven = keep.tile([P, P, PACK], F32, name=tag, align_bytes=64)
             nc.scalar.copy(out=woven[:], in_=turned[:].rearrange("p t j -> p j t"))
             nc.gpsimd.tensor_tensor(
                 rounded(c), woven[:].rearrange("p j t -> p (j t)"), positive[:].rearrange("p j t -> p (j t)"), MULT
@@ -214,18 +219,21 @@ def tile_moe_dub_relu2_kernel(
             )
 
         by_slot = {}
-        by_token = [[keep.tile([P, WINDOW], F32, name=f"by_token{kt}{m}", align_bytes=64) for m in range(2)] for kt in range(K_TILES)]
+        by_token = [[keep.tile([P, T], F32, name=f"by_token{kt}{m}", align_bytes=64) for m in range(2)] for kt in range(K_TILES)]
         lists = (own_list, partner_list)
 
-        def product(into, kt, m, first, count):
+        def product(number, kt, m, first, count, tag=None):
             e, place = divmod(first, C)
             rows = slice(kt * P, (kt + 1) * P)
+            grads = bank(number, [P, count])
+            piece = keep.tile([P, count], F32, name=tag or f"by_slot{kt}{m}{first}", align_bytes=64)
+            by_slot[(kt, m, first)] = piece
             if m == OWN:
                 codes, scales = w1_codes[e][:, rows].bitcast(FP8X4), w1_bytes[4 * e :, rows]
             else:
                 codes, scales = wp_codes[:, e, 2 * kt * P : 2 * (kt + 1) * P].bitcast(FP4X4), wp_bytes[:, e, rows]
             nc.tensor.matmul_mx(
-                out=into,
+                out=grads[:],
                 lhsT=codes,
                 lhsT_scale=scales,
                 rhs=dh_codes[e][:, place : place + count].bitcast(FP8X4),
@@ -233,14 +241,6 @@ def tile_moe_dub_relu2_kernel(
                 start=True,
                 stop=True,
             )
-
-        def products(number, kt, m, first, count, place=None):
-            grads = bank(number, [P, count])
-            piece = keep.tile([P, count], F32, name=place or f"by_slot{kt}{m}{first}", align_bytes=64)
-            by_slot[(kt, m, first)] = piece
-            width = min(count, C)
-            for col in range(0, count, width):
-                product(grads[:, col : col + width], kt, m, first + col, width)
             nc.scalar.copy(out=piece[:], in_=grads[:])
 
         def scatter(kt, m, first, count):
@@ -250,31 +250,31 @@ def tile_moe_dub_relu2_kernel(
 
         def add_on_gpsimd(kt):
             total = keep.tile([P, T], F32, name=f"total{kt}", align_bytes=64)
-            nc.gpsimd.tensor_tensor(total[:], by_token[kt][OWN][:, 0:T], by_token[kt][PARTNER][:, 0:T], ADD)
+            nc.gpsimd.tensor_tensor(total[:], by_token[kt][OWN][:], by_token[kt][PARTNER][:], ADD)
             nc.sync.dma_start(out=out[kt * P : (kt + 1) * P, :], in_=total[:])
 
         def add_on_vector(kt):
             total = keep.tile([P, T], F32, name=f"total{kt}", align_bytes=64)
-            for half in range(2):
-                cols = slice(half * T // 2, (half + 1) * T // 2)
+            for side in range(2):
+                cols = slice(side * T // 2, (side + 1) * T // 2)
                 nc.vector.tensor_tensor(total[:, cols], by_token[kt][OWN][:, cols], by_token[kt][PARTNER][:, cols], ADD)
                 nc.sync.dma_start(out=out[kt * P : (kt + 1) * P, cols], in_=total[:, cols])
 
-        turned0 = hidden_gradient(0, [0, 1], 2)
-        turned1 = hidden_gradient(1, [3], 4)
+        turned0 = gated_sums(0, [0, 1], 2)
+        turned1 = gated_sums(1, [3], 4)
         mask_on_vector(0, turned0, slice(0, HALF))
         quantise(0, HALF)
-        products(5, 0, OWN, 0, HALF)
+        product(5, 0, OWN, 0, HALF)
         mask_on_vector(0, turned0, slice(HALF, P))
         quantise(HALF, HALF)
-        products(6, 1, OWN, 0, P)
-        products(0, 0, OWN, HALF, HALF)
-        mask_on_vector(1, turned1)
+        product(6, 1, OWN, 0, P)
+        product(0, 0, OWN, HALF, HALF)
+        mask_on_vector(1, turned1, slice(0, P))
         quantise(P, P)
-        products(5, 1, OWN, P, P, "late1")
-        products(7, 0, OWN, P, P, "late0")
-        products(6, 2, OWN, 0, C)
-        products(3, 3, OWN, 0, C)
+        product(5, 1, OWN, P, P, "before_positive3")
+        product(7, 0, OWN, P, P, "before_positive2")
+        product(6, 2, OWN, 0, C)
+        product(3, 3, OWN, 0, C)
         scatter(0, OWN, 0, HALF)
         scatter(1, OWN, 0, P)
         scatter(0, OWN, HALF, HALF)
@@ -282,23 +282,25 @@ def tile_moe_dub_relu2_kernel(
         scatter(0, OWN, P, P)
         scatter(2, OWN, 0, C)
         scatter(3, OWN, 0, C)
-        turned2 = hidden_gradient(2, [7], 2)
-        turned3 = hidden_gradient(3, [5], 4)
-        for kt in range(K_TILES - 1):
-            products(6 - 3 * (kt % 2), kt, PARTNER, 0, C)
+
+        turned2 = gated_sums(2, [7], 2)
+        turned3 = gated_sums(3, [5], 4)
+        for kt in range(LAST):
+            product((6, 3)[kt % 2], kt, PARTNER, 0, C)
             scatter(kt, PARTNER, 0, C)
-        mask_on_gpsimd(2, turned2, positive_part(2, "late0"), "woven2")
-        mask_on_gpsimd(3, turned3, positive_part(3, "late1"), "woven3")
+        mask_on_gpsimd(2, turned2, positive_part(2, "before_positive2"), "woven2")
+        mask_on_gpsimd(3, turned3, positive_part(3, "before_positive3"), "woven3")
         quantise(C, C)
-        products(3, 3, PARTNER, 0, C, "woven3")
-        scatter(3, PARTNER, 0, C)
+        product(3, LAST, PARTNER, 0, C, "woven3")
+        scatter(LAST, PARTNER, 0, C)
+
         for kt in range(K_TILES):
-            products(5 + kt % 2, kt, OWN, C, C)
-            products(7 - 5 * (kt % 2), kt, PARTNER, C, C)
-        for kt in range(K_TILES):
+            product((5, 6)[kt % 2], kt, OWN, C, C)
+            product((7, 2)[kt % 2], kt, PARTNER, C, C)
+        for kt in range(LAST):
             scatter(kt, OWN, C, C)
             scatter(kt, PARTNER, C, C)
-            if kt < K_TILES - 1:
-                add_on_gpsimd(kt)
-            else:
-                add_on_vector(kt)
+            add_on_gpsimd(kt)
+        scatter(LAST, OWN, C, C)
+        scatter(LAST, PARTNER, C, C)
+        add_on_vector(LAST)

@@ -16,7 +16,6 @@ U8 = mybir.dt.uint8
 FP8X4 = mybir.dt.float8_e4m3fn_x4
 FP4X4 = mybir.dt.float4_e2m1fn_x4
 COPY = mybir.ActivationFunctionType.Copy
-RELU = mybir.ActivationFunctionType.Relu
 MAX = mybir.AluOpType.max
 MULT = mybir.AluOpType.mult
 ADD = mybir.AluOpType.add
@@ -27,10 +26,7 @@ PASSES = N // (P * PACK)
 K_TILES = K // P
 LAST = K_TILES - 1
 PER_COL = 16
-HALF = P // 2
 OWN, PARTNER = 0, 1
-WARM_UPS = 4
-TWO_ONES = 0x3F803F80
 
 
 def tile_moe_dub_relu2_kernel(
@@ -52,18 +48,13 @@ def tile_moe_dub_relu2_kernel(
         wp_codes = keep.tile([P, E, 2 * K], U8, name="wp_codes", align_bytes=64)
         wp_bytes = keep.tile([P, E, K], U8, name="wp_bytes", align_bytes=64)
         saved = [keep.tile([P, PACK, C], F32, name=f"saved{e}", align_bytes=64) for e in range(E)]
-        gate_col = [keep.tile([P, C // P], F32, name=f"gate_col{e}") for e in range(E)]
-        gate_twice = keep.tile([P, C // P], F32, name="gate_twice")
+        gate_col = keep.tile([P, SLOTS // P], F32, name="gate_col")
+        gate_twice = keep.tile([P, SLOTS // P], F32, name="gate_twice")
         identity = keep.tile([P, P], F32, name="identity", align_bytes=64)
 
         make_identity(nc, identity[:])
         nc.vector.memset(dy_bytes[:].bitcast(I32), 0)
         nc.vector.memset(w2_bytes[:].bitcast(I32), 0)
-        ones = keep.tile([P, PACK * H], BF16, name="ones", align_bytes=64)
-        warm_codes = keep.tile([P, H], U32, name="warm_codes", align_bytes=64)
-        warm_bytes = keep.tile([P, H], U8, name="warm_bytes", align_bytes=64)
-        nc.vector.memset(ones[:].bitcast(I32), TWO_ONES)
-        nc.vector.quantize_mx(out=warm_codes[:].bitcast(FP8X4), scales=warm_bytes[:], in_=ones[:])
         nc.vector.memset(w1_bytes[:].bitcast(I32), 0)
         nc.vector.memset(wp_bytes[:].rearrange("p e k -> p (e k)").bitcast(I32), 0)
 
@@ -81,9 +72,9 @@ def tile_moe_dub_relu2_kernel(
         def load_dy(s):
             nc.sync.dma_start(out=dy_codes[:, s * T : (s + 1) * T], in_=dy_words[s].rearrange("p t d -> p (t d)").bitcast(I32))
 
-        def load_gate(e):
+        def load_gate():
             with nc.allow_non_contiguous_dma(reason="one gate value a partition and chunk"):
-                nc.sync.dma_start(out=gate_col[e][:], in_=gate[0:1, e * C : (e + 1) * C].rearrange("o (c p) -> p (o c)", p=P))
+                nc.sync.dma_start(out=gate_col[:], in_=gate[0:1, :].rearrange("o (c p) -> p (o c)", p=P))
 
         def load_w1(e):
             nc.sync.dma_start(out=w1_codes[e][:], in_=w1t_words[e, 0].rearrange("p k d -> p (k d)").bitcast(I32))
@@ -97,10 +88,12 @@ def tile_moe_dub_relu2_kernel(
         load_dy(1)
         load_w2(0)
         load_planes(w2_bytes, w2t_scales.rearrange("e s b i -> (e s) b i"))
-        load_gate(0)
+        load_gate()
+        load_w2(1)
         load_saved(0)
         load_w1(0)
         load_planes(w1_bytes, w1t_scales.rearrange("e s b k -> (e s) b k"))
+        load_saved(1)
         nc.sync.dma_start(out=wp_codes[:].bitcast(I32), in_=wpt_words.rearrange("e s p b -> p (e s) b").bitcast(I32))
         nc.sync.dma_start(partner_list[:], offs2)
         wp_rows = wpt_scales.rearrange("e s b k -> b (e s) k")
@@ -109,28 +102,12 @@ def tile_moe_dub_relu2_kernel(
                 out=wp_bytes[32 * q : 32 * q + 4, :, :].bitcast(I32),
                 in_=wp_rows[4 * q : 4 * q + 4, :, :].bitcast(I32),
             )
-        load_gate(1)
-        load_w2(1)
-        load_saved(1)
         load_w1(1)
 
         def bank(number, shape):
             return psum.tile(shape, F32, name=f"bank{number}")
 
-        nc.scalar.mul(gate_twice[:], gate_col[0][:], 2.0)
-        gate_scale = (gate_twice, gate_col[1])
-
-        warm = bank(6, [P, H])
-        for n in range(WARM_UPS):
-            nc.tensor.matmul_mx(
-                out=warm[:],
-                lhsT=warm_codes[:, 0:P].bitcast(FP8X4),
-                lhsT_scale=warm_bytes[:, 0:P],
-                rhs=warm_codes[:].bitcast(FP8X4),
-                rhs_scale=warm_bytes[:],
-                start=True,
-                stop=True,
-            )
+        nc.scalar.mul(gate_twice[:], gate_col[:], 2.0)
 
         def list_cols(first, count):
             return slice(first // PER_COL, (first + count) // PER_COL)
@@ -172,7 +149,7 @@ def tile_moe_dub_relu2_kernel(
                     out=gated[:, :, part * width // PACK : (part + 1) * width // PACK],
                     in_=sums.rearrange("j (m t) -> j t m", t=PACK),
                     func=COPY,
-                    scale=gate_scale[e][:, within : within + 1],
+                    scale=gate_twice[:, c : c + 1],
                 )
             turned = bank(turned_bank, [P, PACK, P])
             for t in range(PACK):
@@ -187,26 +164,14 @@ def tile_moe_dub_relu2_kernel(
             e, within = divmod(c, C // P)
             return saved[e][:, :, within * P : (within + 1) * P].rearrange("p t j -> p j t")
 
-        def mask_on_vector(c, turned, slots):
+        def mask(c, turned):
             nc.vector.scalar_tensor_tensor(
-                out=rounded(c).rearrange("p (j t) -> p j t", t=PACK)[:, slots, :],
-                in0=saved_by_slot(c)[:, slots, :],
+                out=rounded(c).rearrange("p (j t) -> p j t", t=PACK),
+                in0=saved_by_slot(c),
                 scalar=0.0,
-                in1=turned[:].rearrange("p t j -> p j t")[:, slots, :],
+                in1=turned[:].rearrange("p t j -> p j t"),
                 op0=MAX,
                 op1=MULT,
-            )
-
-        def positive_part(c, tag):
-            positive = keep.tile([P, P, PACK], F32, name=tag, align_bytes=64)
-            nc.scalar.activation(out=positive[:], in_=saved_by_slot(c), func=RELU, scale=2.0)
-            return positive
-
-        def mask_on_gpsimd(c, turned, positive, tag):
-            woven = keep.tile([P, P, PACK], F32, name=tag, align_bytes=64)
-            nc.scalar.copy(out=woven[:], in_=turned[:].rearrange("p t j -> p j t"))
-            nc.gpsimd.tensor_tensor(
-                rounded(c), woven[:].rearrange("p j t -> p (j t)"), positive[:].rearrange("p j t -> p (j t)"), MULT
             )
 
         def quantise(first, count):
@@ -218,22 +183,18 @@ def tile_moe_dub_relu2_kernel(
                 in_=dh[e][:, PACK * place : PACK * (place + count)],
             )
 
-        by_slot = {}
         by_token = [[keep.tile([P, T], F32, name=f"by_token{kt}{m}", align_bytes=64) for m in range(2)] for kt in range(K_TILES)]
         lists = (own_list, partner_list)
 
-        def product(number, kt, m, first, count, tag=None):
+        def product(grads, kt, m, first, count):
             e, place = divmod(first, C)
             rows = slice(kt * P, (kt + 1) * P)
-            grads = bank(number, [P, count])
-            piece = keep.tile([P, count], F32, name=tag or f"by_slot{kt}{m}{first}", align_bytes=64)
-            by_slot[(kt, m, first)] = piece
             if m == OWN:
                 codes, scales = w1_codes[e][:, rows].bitcast(FP8X4), w1_bytes[4 * e :, rows]
             else:
                 codes, scales = wp_codes[:, e, 2 * kt * P : 2 * (kt + 1) * P].bitcast(FP4X4), wp_bytes[:, e, rows]
             nc.tensor.matmul_mx(
-                out=grads[:],
+                out=grads,
                 lhsT=codes,
                 lhsT_scale=scales,
                 rhs=dh_codes[e][:, place : place + count].bitcast(FP8X4),
@@ -241,12 +202,35 @@ def tile_moe_dub_relu2_kernel(
                 start=True,
                 stop=True,
             )
-            nc.scalar.copy(out=piece[:], in_=grads[:])
 
-        def scatter(kt, m, first, count):
-            nc.vector.tensor_copy(
-                by_token[kt][m][:].indirect(lists[m][:, list_cols(first, count)]), by_slot[(kt, m, first)][:]
-            )
+        def to_sbuf(grads, name, on_vector):
+            piece = keep.tile(list(grads.shape), F32, name=name, align_bytes=64)
+            if on_vector:
+                nc.vector.tensor_copy(piece[:], grads[:])
+            else:
+                nc.scalar.copy(out=piece[:], in_=grads[:])
+            return piece
+
+        def scatter(values, kt, m, first, count):
+            window = by_token[kt][m][:].indirect(lists[m][:, list_cols(first, count)])
+            if m == OWN:
+                nc.scalar.activation(out=window, in_=values, func=COPY)
+            else:
+                nc.vector.tensor_copy(window, values)
+
+        def early(number, m, tiles):
+            grads = bank(number, [P, len(tiles) * P])
+            for place, kt in enumerate(tiles):
+                product(grads[:, place * P : (place + 1) * P], kt, m, 0, P)
+            piece = to_sbuf(grads, f"early{m}{tiles[0]}", m == PARTNER)
+            for place, kt in enumerate(tiles):
+                scatter(piece[:, place * P : (place + 1) * P], kt, m, 0, P)
+
+        def late(number, m, kt, on_vector):
+            grads = bank(number, [P, SLOTS - P])
+            product(grads[:, 0 : C - P], kt, m, P, C - P)
+            product(grads[:, C - P :], kt, m, C, C)
+            return to_sbuf(grads, f"late{m}{kt}", on_vector)
 
         def add_on_gpsimd(kt):
             total = keep.tile([P, T], F32, name=f"total{kt}", align_bytes=64)
@@ -260,47 +244,23 @@ def tile_moe_dub_relu2_kernel(
                 nc.vector.tensor_tensor(total[:, cols], by_token[kt][OWN][:, cols], by_token[kt][PARTNER][:, cols], ADD)
                 nc.sync.dma_start(out=out[kt * P : (kt + 1) * P, cols], in_=total[:, cols])
 
-        turned0 = gated_sums(0, [0, 1], 2)
-        turned1 = gated_sums(1, [3], 4)
-        mask_on_vector(0, turned0, slice(0, HALF))
-        quantise(0, HALF)
-        product(5, 0, OWN, 0, HALF)
-        mask_on_vector(0, turned0, slice(HALF, P))
-        quantise(HALF, HALF)
-        product(6, 1, OWN, 0, P)
-        product(0, 0, OWN, HALF, HALF)
-        mask_on_vector(1, turned1, slice(0, P))
+        turned = [gated_sums(0, [0, 1], 5), gated_sums(1, [2], 6), gated_sums(2, [3], 7), gated_sums(3, [4], 0)]
+        mask(0, turned[0])
+        quantise(0, P)
+        early(1, OWN, range(K_TILES))
+        mask(1, turned[1])
         quantise(P, P)
-        product(5, 1, OWN, P, P, "before_positive3")
-        product(7, 0, OWN, P, P, "before_positive2")
-        product(6, 2, OWN, 0, C)
-        product(3, 3, OWN, 0, C)
-        scatter(0, OWN, 0, HALF)
-        scatter(1, OWN, 0, P)
-        scatter(0, OWN, HALF, HALF)
-        scatter(1, OWN, P, P)
-        scatter(0, OWN, P, P)
-        scatter(2, OWN, 0, C)
-        scatter(3, OWN, 0, C)
-
-        turned2 = gated_sums(2, [7], 2)
-        turned3 = gated_sums(3, [5], 4)
-        for kt in range(LAST):
-            product((6, 3)[kt % 2], kt, PARTNER, 0, C)
-            scatter(kt, PARTNER, 0, C)
-        mask_on_gpsimd(2, turned2, positive_part(2, "before_positive2"), "woven2")
-        mask_on_gpsimd(3, turned3, positive_part(3, "before_positive3"), "woven3")
+        mask(2, turned[2])
+        mask(3, turned[3])
         quantise(C, C)
-        product(3, LAST, PARTNER, 0, C, "woven3")
-        scatter(LAST, PARTNER, 0, C)
-
+        early(2, PARTNER, range(K_TILES))
+        own_banks, partner_banks = (3, 5, 7, 1), (4, 6, 0, 2)
         for kt in range(K_TILES):
-            product((5, 6)[kt % 2], kt, OWN, C, C)
-            product((7, 2)[kt % 2], kt, PARTNER, C, C)
-        for kt in range(LAST):
-            scatter(kt, OWN, C, C)
-            scatter(kt, PARTNER, C, C)
-            add_on_gpsimd(kt)
-        scatter(LAST, OWN, C, C)
-        scatter(LAST, PARTNER, C, C)
-        add_on_vector(LAST)
+            own = late(own_banks[kt], OWN, kt, False)
+            partner = late(partner_banks[kt], PARTNER, kt, kt < 1)
+            scatter(own[:], kt, OWN, P, SLOTS - P)
+            scatter(partner[:], kt, PARTNER, P, SLOTS - P)
+            if kt < LAST:
+                add_on_gpsimd(kt)
+            else:
+                add_on_vector(kt)

@@ -127,7 +127,7 @@ def tile_moe_dub_relu2_kernel(
         dh_codes = [keep.tile([P, C], U32, name=f"dh_codes{e}", align_bytes=64) for e in range(E)]
         dh_bytes = [keep.tile([P, C], U8, name=f"dh_bytes{e}", align_bytes=64) for e in range(E)]
 
-        def gated_sums(c, sums_banks, turned_bank):
+        def gated_sums(c, sums_banks):
             e, within = divmod(c, C // P)
             cols = slice(within * P, (within + 1) * P)
             gated = keep.tile([P, PACK, P], F32, name=f"gated{c}", align_bytes=64)
@@ -151,7 +151,10 @@ def tile_moe_dub_relu2_kernel(
                     func=COPY,
                     scale=gate_twice[:, c : c + 1],
                 )
-            turned = bank(turned_bank, [P, PACK, P])
+            return gated
+
+        def turn(gated, number):
+            turned = bank(number, [P, PACK, P])
             for t in range(PACK):
                 nc.tensor.transpose(turned[:, t, :], gated[:, t, :], identity[:])
             return turned
@@ -164,10 +167,17 @@ def tile_moe_dub_relu2_kernel(
             e, within = divmod(c, C // P)
             return saved[e][:, :, within * P : (within + 1) * P].rearrange("p t j -> p j t")
 
+        def woven(c):
+            if c == 0:
+                return saved_by_slot(c)
+            values = keep.tile([P, P, PACK], F32, name=f"woven{c}", align_bytes=64)
+            nc.gpsimd.tensor_copy(values[:], saved_by_slot(c))
+            return values[:]
+
         def mask(c, turned):
             nc.vector.scalar_tensor_tensor(
                 out=rounded(c).rearrange("p (j t) -> p j t", t=PACK),
-                in0=saved_by_slot(c),
+                in0=woven(c),
                 scalar=0.0,
                 in1=turned[:].rearrange("p t j -> p j t"),
                 op0=MAX,
@@ -244,22 +254,26 @@ def tile_moe_dub_relu2_kernel(
                 nc.vector.tensor_tensor(total[:, cols], by_token[kt][OWN][:, cols], by_token[kt][PARTNER][:, cols], ADD)
                 nc.sync.dma_start(out=out[kt * P : (kt + 1) * P, cols], in_=total[:, cols])
 
-        turned = [gated_sums(0, [0, 1], 5), gated_sums(1, [2], 6), gated_sums(2, [3], 7), gated_sums(3, [4], 0)]
-        mask(0, turned[0])
+        gated0 = gated_sums(0, [0, 1])
+        turned0 = turn(gated0, 4)
+        gated1 = gated_sums(1, [2])
+        gated2 = gated_sums(2, [1])
+        gated3 = gated_sums(3, [3])
+        mask(0, turned0)
         quantise(0, P)
-        early(1, OWN, range(K_TILES))
-        mask(1, turned[1])
+        early(7, OWN, range(K_TILES))
+        mask(1, turn(gated1, 1))
         quantise(P, P)
-        mask(2, turned[2])
-        mask(3, turned[3])
+        mask(2, turn(gated2, 5))
+        mask(3, turn(gated3, 6))
         quantise(C, C)
-        early(2, PARTNER, range(K_TILES))
-        own_banks, partner_banks = (3, 5, 7, 1), (4, 6, 0, 2)
+        early(6, PARTNER, range(K_TILES))
+        own_banks, partner_banks = (3, 4, 7, 5), (0, 2, 1, 6)
+        partner = [late(partner_banks[kt], PARTNER, kt, kt == LAST) for kt in range(K_TILES)]
+        own = [late(own_banks[kt], OWN, kt, False) for kt in range(K_TILES)]
         for kt in range(K_TILES):
-            own = late(own_banks[kt], OWN, kt, False)
-            partner = late(partner_banks[kt], PARTNER, kt, kt < 1)
-            scatter(own[:], kt, OWN, P, SLOTS - P)
-            scatter(partner[:], kt, PARTNER, P, SLOTS - P)
+            scatter(own[kt][:], kt, OWN, P, SLOTS - P)
+            scatter(partner[kt][:], kt, PARTNER, P, SLOTS - P)
             if kt < LAST:
                 add_on_gpsimd(kt)
             else:

@@ -48,12 +48,14 @@ def tile_moe_dub_relu2_kernel(
         wp_codes = keep.tile([P, E, 2 * K], U8, name="wp_codes", align_bytes=64)
         wp_bytes = keep.tile([P, E, K], U8, name="wp_bytes", align_bytes=64)
         saved = [keep.tile([P, PACK, C], F32, name=f"saved{e}", align_bytes=64) for e in range(E)]
-        gate_col = keep.tile([P, SLOTS // P], F32, name="gate_col")
+        gate_rows = keep.tile([P, P], F32, name="gate_rows", align_bytes=64)
         gate_twice = keep.tile([P, SLOTS // P], F32, name="gate_twice")
         identity = keep.tile([P, P], F32, name="identity", align_bytes=64)
 
+        nc.gpsimd.memset(dy_bytes[:].bitcast(I32), 0)
+        nc.gpsimd.memset(gate_rows[:], 0.0)
+        nc.gpsimd.dma_start(out=gate_rows[0 : SLOTS // P, :], in_=gate[0:1, :].rearrange("o (c p) -> (o c) p", p=P))
         make_identity(nc, identity[:])
-        nc.vector.memset(dy_bytes[:].bitcast(I32), 0)
         nc.vector.memset(w2_bytes[:].bitcast(I32), 0)
         nc.vector.memset(w1_bytes[:].bitcast(I32), 0)
         nc.vector.memset(wp_bytes[:].rearrange("p e k -> p (e k)").bitcast(I32), 0)
@@ -72,10 +74,6 @@ def tile_moe_dub_relu2_kernel(
         def load_dy(s):
             nc.sync.dma_start(out=dy_codes[:, s * T : (s + 1) * T], in_=dy_words[s].rearrange("p t d -> p (t d)").bitcast(I32))
 
-        def load_gate():
-            with nc.allow_non_contiguous_dma(reason="one gate value a partition and chunk"):
-                nc.sync.dma_start(out=gate_col[:], in_=gate[0:1, :].rearrange("o (c p) -> p (o c)", p=P))
-
         def load_w1(e):
             nc.sync.dma_start(out=w1_codes[e][:], in_=w1t_words[e, 0].rearrange("p k d -> p (k d)").bitcast(I32))
 
@@ -88,7 +86,6 @@ def tile_moe_dub_relu2_kernel(
         load_dy(1)
         load_w2(0)
         load_planes(w2_bytes, w2t_scales.rearrange("e s b i -> (e s) b i"))
-        load_gate()
         load_w2(1)
         load_saved(0)
         load_w1(0)
@@ -107,7 +104,9 @@ def tile_moe_dub_relu2_kernel(
         def bank(number, shape):
             return psum.tile(shape, F32, name=f"bank{number}")
 
-        nc.scalar.mul(gate_twice[:], gate_col[:], 2.0)
+        gate_cols = bank(5, [P, P])
+        nc.tensor.transpose(gate_cols[:], gate_rows[:], identity[:])
+        nc.scalar.mul(gate_twice[:], gate_cols[:, 0 : SLOTS // P], 2.0)
 
         def list_cols(first, count):
             return slice(first // PER_COL, (first + count) // PER_COL)
@@ -221,20 +220,20 @@ def tile_moe_dub_relu2_kernel(
                 nc.scalar.copy(out=piece[:], in_=grads[:])
             return piece
 
-        def scatter(values, kt, m, first, count):
+        def scatter(values, kt, m, first, count, on_vector):
             window = by_token[kt][m][:].indirect(lists[m][:, list_cols(first, count)])
-            if m == OWN:
-                nc.scalar.activation(out=window, in_=values, func=COPY)
-            else:
+            if on_vector:
                 nc.vector.tensor_copy(window, values)
+            else:
+                nc.scalar.activation(out=window, in_=values, func=COPY)
 
-        def early(number, m, tiles):
+        def early(number, m, tiles, on_vector):
             grads = bank(number, [P, len(tiles) * P])
             for place, kt in enumerate(tiles):
                 product(grads[:, place * P : (place + 1) * P], kt, m, 0, P)
-            piece = to_sbuf(grads, f"early{m}{tiles[0]}", m == PARTNER)
+            piece = to_sbuf(grads, f"early{m}{tiles[0]}", on_vector)
             for place, kt in enumerate(tiles):
-                scatter(piece[:, place * P : (place + 1) * P], kt, m, 0, P)
+                scatter(piece[:, place * P : (place + 1) * P], kt, m, 0, P, on_vector)
 
         def late(number, m, kt, on_vector):
             grads = bank(number, [P, SLOTS - P])
@@ -261,19 +260,23 @@ def tile_moe_dub_relu2_kernel(
         gated3 = gated_sums(3, [3])
         mask(0, turned0)
         quantise(0, P)
-        early(7, OWN, range(K_TILES))
-        mask(1, turn(gated1, 1))
+        turned1 = turn(gated1, 4)
+        early(7, OWN, (0, 1), False)
+        early(5, OWN, (2,), False)
+        mask(1, turned1)
         quantise(P, P)
-        mask(2, turn(gated2, 5))
+        early(6, OWN, (3,), True)
+        mask(2, turn(gated2, 7))
         mask(3, turn(gated3, 6))
         quantise(C, C)
-        early(6, PARTNER, range(K_TILES))
-        own_banks, partner_banks = (3, 4, 7, 5), (0, 2, 1, 6)
-        partner = [late(partner_banks[kt], PARTNER, kt, kt == LAST) for kt in range(K_TILES)]
-        own = [late(own_banks[kt], OWN, kt, False) for kt in range(K_TILES)]
-        for kt in range(K_TILES):
-            scatter(own[kt][:], kt, OWN, P, SLOTS - P)
-            scatter(partner[kt][:], kt, PARTNER, P, SLOTS - P)
+        early(0, PARTNER, (0,), False)
+        early(6, PARTNER, (1, 2, 3), True)
+        own_banks, partner_banks = (5, 4, 7, 0), (1, 2, 3, 6)
+        partners = [late(partner_banks[kt], PARTNER, kt, kt == LAST) for kt in range(K_TILES)]
+        owns = [late(own_banks[kt], OWN, kt, False) for kt in range(K_TILES)]
+        for kt, (own, partner) in enumerate(zip(owns, partners)):
+            scatter(own[:], kt, OWN, P, SLOTS - P, False)
+            scatter(partner[:], kt, PARTNER, P, SLOTS - P, True)
             if kt < LAST:
                 add_on_gpsimd(kt)
             else:

@@ -43,7 +43,7 @@ def tile_moe_dub_relu2_kernel(
         dy_bytes = keep.tile([P, T], U8, name="dy_bytes", align_bytes=64)
         w2_codes = [keep.tile([P, PASSES, H], I32, name=f"w2_codes{e}", align_bytes=64) for e in range(E)]
         w2_bytes = keep.tile([P, H], U8, name="w2_bytes", align_bytes=64)
-        w1_codes = [keep.tile([P, K], I32, name=f"w1_codes{e}", align_bytes=64) for e in range(E)]
+        w1_codes = keep.tile([P, E, K], I32, name="w1_codes", align_bytes=64)
         w1_bytes = keep.tile([P, K], U8, name="w1_bytes", align_bytes=64)
         wp_codes = keep.tile([P, E, 2 * K], U8, name="wp_codes", align_bytes=64)
         wp_bytes = keep.tile([P, E, K], U8, name="wp_bytes", align_bytes=64)
@@ -56,9 +56,15 @@ def tile_moe_dub_relu2_kernel(
         nc.gpsimd.memset(gate_rows[:], 0.0)
         nc.gpsimd.dma_start(out=gate_rows[0 : SLOTS // P, :], in_=gate[0:1, :].rearrange("o (c p) -> (o c) p", p=P))
         make_identity(nc, identity[:])
+        nc.gpsimd.memset(wp_bytes[:].rearrange("p e k -> p (e k)").bitcast(I32), 0)
+        wp_rows = wpt_scales.rearrange("e s b k -> b (e s) k")
+        for q in range(4):
+            nc.gpsimd.dma_start(
+                out=wp_bytes[32 * q : 32 * q + 4, :, :].bitcast(I32),
+                in_=wp_rows[4 * q : 4 * q + 4, :, :].bitcast(I32),
+            )
         nc.vector.memset(w2_bytes[:].bitcast(I32), 0)
         nc.vector.memset(w1_bytes[:].bitcast(I32), 0)
-        nc.vector.memset(wp_bytes[:].rearrange("p e k -> p (e k)").bitcast(I32), 0)
 
         def load_planes(plane, rows):
             count = rows.shape[0]
@@ -74,9 +80,6 @@ def tile_moe_dub_relu2_kernel(
         def load_dy(s):
             nc.sync.dma_start(out=dy_codes[:, s * T : (s + 1) * T], in_=dy_words[s].rearrange("p t d -> p (t d)").bitcast(I32))
 
-        def load_w1(e):
-            nc.sync.dma_start(out=w1_codes[e][:], in_=w1t_words[e, 0].rearrange("p k d -> p (k d)").bitcast(I32))
-
         def load_saved(e):
             nc.sync.dma_start(out=saved[e][:], in_=a[:, e * C : (e + 1) * C].rearrange("(p t) j -> p t j", t=PACK))
 
@@ -88,18 +91,11 @@ def tile_moe_dub_relu2_kernel(
         load_planes(w2_bytes, w2t_scales.rearrange("e s b i -> (e s) b i"))
         load_w2(1)
         load_saved(0)
-        load_w1(0)
+        nc.sync.dma_start(out=w1_codes[:], in_=w1t_words.rearrange("e s p k d -> p (e s) (k d)").bitcast(I32))
         load_planes(w1_bytes, w1t_scales.rearrange("e s b k -> (e s) b k"))
         load_saved(1)
         nc.sync.dma_start(out=wp_codes[:].bitcast(I32), in_=wpt_words.rearrange("e s p b -> p (e s) b").bitcast(I32))
         nc.sync.dma_start(partner_list[:], offs2)
-        wp_rows = wpt_scales.rearrange("e s b k -> b (e s) k")
-        for q in range(4):
-            nc.sync.dma_start(
-                out=wp_bytes[32 * q : 32 * q + 4, :, :].bitcast(I32),
-                in_=wp_rows[4 * q : 4 * q + 4, :, :].bitcast(I32),
-            )
-        load_w1(1)
 
         def bank(number, shape):
             return psum.tile(shape, F32, name=f"bank{number}")
@@ -199,7 +195,7 @@ def tile_moe_dub_relu2_kernel(
             e, place = divmod(first, C)
             rows = slice(kt * P, (kt + 1) * P)
             if m == OWN:
-                codes, scales = w1_codes[e][:, rows].bitcast(FP8X4), w1_bytes[4 * e :, rows]
+                codes, scales = w1_codes[:, e, rows].bitcast(FP8X4), w1_bytes[4 * e :, rows]
             else:
                 codes, scales = wp_codes[:, e, 2 * kt * P : 2 * (kt + 1) * P].bitcast(FP4X4), wp_bytes[:, e, rows]
             nc.tensor.matmul_mx(

@@ -41,20 +41,21 @@ def tile_moe_dub_relu2_kernel(
         partner_list = keep.tile([P, SLOTS // PER_COL], U16, name="partner_list")
         dy_codes = keep.tile([P, PASSES * T], I32, name="dy_codes", align_bytes=64)
         dy_bytes = keep.tile([P, T], U8, name="dy_bytes", align_bytes=64)
-        w2_codes = [keep.tile([P, PASSES, H], I32, name=f"w2_codes{e}", align_bytes=64) for e in range(E)]
+        w2_first = [keep.tile([P, H], I32, name=f"w2_first{s}", align_bytes=64) for s in range(PASSES)]
+        w2_second = keep.tile([P, PASSES, H], I32, name="w2_second", align_bytes=64)
+        w2_codes = [[w2_first[s][:] for s in range(PASSES)], [w2_second[:, s, :] for s in range(PASSES)]]
         w2_bytes = keep.tile([P, H], U8, name="w2_bytes", align_bytes=64)
-        w1_codes = keep.tile([P, E, K], I32, name="w1_codes", align_bytes=64)
+        w1_codes = [keep.tile([P, K], I32, name=f"w1_codes{e}", align_bytes=64) for e in range(E)]
         w1_bytes = keep.tile([P, K], U8, name="w1_bytes", align_bytes=64)
         wp_codes = keep.tile([P, E, 2 * K], U8, name="wp_codes", align_bytes=64)
         wp_bytes = keep.tile([P, E, K], U8, name="wp_bytes", align_bytes=64)
         saved = [keep.tile([P, PACK, C], F32, name=f"saved{e}", align_bytes=64) for e in range(E)]
-        gate_rows = keep.tile([P, P], F32, name="gate_rows", align_bytes=64)
+        gate_rows = keep.tile([P, 32], F32, name="gate_rows", tag="gate_rows", align_bytes=64)
         gate_twice = keep.tile([P, SLOTS // P], F32, name="gate_twice")
         identity = keep.tile([P, P], F32, name="identity", align_bytes=64)
 
         nc.gpsimd.memset(dy_bytes[:].bitcast(I32), 0)
-        nc.gpsimd.memset(gate_rows[:], 0.0)
-        nc.gpsimd.dma_start(out=gate_rows[0 : SLOTS // P, :], in_=gate[0:1, :].rearrange("o (c p) -> (o c) p", p=P))
+        nc.gpsimd.dma_start(out=gate_rows[:], in_=gate[0:8, :].rearrange("o (c q x) -> q (o c) x", c=4, q=4))
         make_identity(nc, identity[:])
         nc.gpsimd.memset(wp_bytes[:].rearrange("p e k -> p (e k)").bitcast(I32), 0)
         wp_rows = wpt_scales.rearrange("e s b k -> b (e s) k")
@@ -74,8 +75,9 @@ def tile_moe_dub_relu2_kernel(
                     in_=rows[:, 4 * q : 4 * q + 4, :].bitcast(I32),
                 )
 
-        def load_w2(e):
-            nc.sync.dma_start(out=w2_codes[e][:], in_=w2t_words[e].rearrange("s p i d -> p s (i d)").bitcast(I32))
+
+        def load_w1(e):
+            nc.sync.dma_start(out=w1_codes[e][:], in_=w1t_words[e, 0].rearrange("p k d -> p (k d)").bitcast(I32))
 
         def load_dy(s):
             nc.sync.dma_start(out=dy_codes[:, s * T : (s + 1) * T], in_=dy_words[s].rearrange("p t d -> p (t d)").bitcast(I32))
@@ -87,155 +89,120 @@ def tile_moe_dub_relu2_kernel(
         load_dy(0)
         load_planes(dy_bytes, dy_scales)
         load_dy(1)
-        load_w2(0)
+        nc.sync.dma_start(out=w2_codes[0][0], in_=w2t_words[0, 0].rearrange("p i d -> p (i d)").bitcast(I32))
         load_planes(w2_bytes, w2t_scales.rearrange("e s b i -> (e s) b i"))
-        load_w2(1)
+        nc.sync.dma_start(out=w2_codes[0][1], in_=w2t_words[0, 1].rearrange("p i d -> p (i d)").bitcast(I32))
         load_saved(0)
-        nc.sync.dma_start(out=w1_codes[:], in_=w1t_words.rearrange("e s p k d -> p (e s) (k d)").bitcast(I32))
+        nc.sync.dma_start(out=w2_second[:], in_=w2t_words[1].rearrange("s p i d -> p s (i d)").bitcast(I32))
+        load_w1(0)
         load_planes(w1_bytes, w1t_scales.rearrange("e s b k -> (e s) b k"))
         load_saved(1)
         nc.sync.dma_start(out=wp_codes[:].bitcast(I32), in_=wpt_words.rearrange("e s p b -> p (e s) b").bitcast(I32))
         nc.sync.dma_start(partner_list[:], offs2)
+        load_w1(1)
 
         def bank(number, shape):
             return psum.tile(shape, F32, name=f"bank{number}")
 
-        gate_cols = bank(5, [P, P])
-        nc.tensor.transpose(gate_cols[:], gate_rows[:], identity[:])
-        nc.scalar.mul(gate_twice[:], gate_cols[:, 0 : SLOTS // P], 2.0)
 
         def list_cols(first, count):
             return slice(first // PER_COL, (first + count) // PER_COL)
 
-        g_codes = [[keep.tile([P, C], U32, name=f"g_codes{e}{s}", align_bytes=64) for s in range(PASSES)] for e in range(E)]
-        g_bytes = [keep.tile([P, C], U8, name=f"g_bytes{e}", align_bytes=64) for e in range(E)]
-        for first, count in ((0, P), (P, P), (C, C)):
-            e, place = divmod(first, C)
-            picks = own_list[:, list_cols(first, count)]
-            for s in range(PASSES):
-                end = T if (first, s) == (0, 0) else PASSES * T
-                window = dy_codes[:, s * T : end].bitcast(U32)
-                nc.vector.tensor_copy(g_codes[e][s][:, place : place + count], window.indirect(picks))
-            nc.vector.tensor_copy(g_bytes[e][:, place : place + count], dy_bytes[:].indirect(picks))
+        def gather(dtype, name, window, first, count, tag):
+            picked = keep.tile([P, count], dtype, name=name, tag=tag, align_bytes=64)
+            nc.vector.tensor_copy(picked[:], window.indirect(own_list[:, list_cols(first, count)]))
+            return picked
+
+        words = dy_codes[:].bitcast(U32)
+        pass0 = [gather(U32, f"g0{c}", words[:, 0:T], c * P, P, f"g0{c}") for c in range(2)]
+        bytes0 = gather(U8, "bytes0", dy_bytes[:], 0, C, "bytes0")
+        pass1 = gather(U32, "g1", words[:, T:], 0, C, "g1")
+        late0 = gather(U32, "late0", words, C, C, "late0")
+        late1 = gather(U32, "late1", words[:, T:], C, C, "late1")
 
         dh = [keep.tile([P, C * PACK], BF16, name=f"dh{e}", align_bytes=64) for e in range(E)]
         dh_codes = [keep.tile([P, C], U32, name=f"dh_codes{e}", align_bytes=64) for e in range(E)]
         dh_bytes = [keep.tile([P, C], U8, name=f"dh_bytes{e}", align_bytes=64) for e in range(E)]
 
-        def gated_sums(c, sums_banks):
+        def gated_sums(c, number, codes, scales):
             e, within = divmod(c, C // P)
             cols = slice(within * P, (within + 1) * P)
             gated = keep.tile([P, PACK, P], F32, name=f"gated{c}", align_bytes=64)
-            width = H // len(sums_banks)
-            for part, number in enumerate(sums_banks):
-                hidden = slice(part * width, (part + 1) * width)
-                sums = bank(number, [P, width])[:]
-                for s in range(PASSES):
-                    nc.tensor.matmul_mx(
-                        out=sums,
-                        lhsT=g_codes[e][s][:, cols].bitcast(FP8X4),
-                        lhsT_scale=g_bytes[e][4 * s :, cols],
-                        rhs=w2_codes[e][:, s, hidden].bitcast(FP8X4),
-                        rhs_scale=w2_bytes[4 * (PASSES * e + s) :, hidden],
-                        start=(s == 0),
-                        stop=(s == PASSES - 1),
-                    )
-                nc.scalar.activation(
-                    out=gated[:, :, part * width // PACK : (part + 1) * width // PACK],
-                    in_=sums.rearrange("j (m t) -> j t m", t=PACK),
-                    func=COPY,
-                    scale=gate_twice[:, c : c + 1],
+            sums = bank(number, [P, H])[:]
+            for s in range(PASSES):
+                nc.tensor.matmul_mx(
+                    out=sums,
+                    lhsT=codes[s].bitcast(FP8X4),
+                    lhsT_scale=scales[4 * s :, cols],
+                    rhs=w2_codes[e][s].bitcast(FP8X4),
+                    rhs_scale=w2_bytes[4 * (PASSES * e + s) :, :],
+                    start=(s == 0),
+                    stop=(s == PASSES - 1),
                 )
+            if c == 0:
+                gate_cols = keep.tile([P, 32], F32, name="gate_cols", tag="g00", align_bytes=64)
+                nc.vector.transpose(gate_cols[:], gate_rows[:])
+                nc.scalar.mul(gate_twice[:], gate_cols[:, 0 : SLOTS // P], 2.0)
+            nc.scalar.activation(
+                out=gated[:],
+                in_=sums.rearrange("j (m t) -> j t m", t=PACK),
+                func=COPY,
+                scale=gate_twice[:, c : c + 1],
+            )
             return gated
 
-        def turn(gated, number):
+        def masked(c, gated, number):
+            e, within = divmod(c, C // P)
             turned = bank(number, [P, PACK, P])
             for t in range(PACK):
                 nc.tensor.transpose(turned[:, t, :], gated[:, t, :], identity[:])
-            return turned
-
-        def rounded(c):
-            e, within = divmod(c, C // P)
-            return dh[e][:, within * P * PACK : (within + 1) * P * PACK]
-
-        def saved_by_slot(c):
-            e, within = divmod(c, C // P)
-            return saved[e][:, :, within * P : (within + 1) * P].rearrange("p t j -> p j t")
-
-        def woven(c):
-            if c == 0:
-                return saved_by_slot(c)
-            values = keep.tile([P, P, PACK], F32, name=f"woven{c}", align_bytes=64)
-            nc.gpsimd.tensor_copy(values[:], saved_by_slot(c))
-            return values[:]
-
-        def mask(c, turned):
             nc.vector.scalar_tensor_tensor(
-                out=rounded(c).rearrange("p (j t) -> p j t", t=PACK),
-                in0=woven(c),
+                out=dh[e][:, within * P * PACK : (within + 1) * P * PACK].rearrange("p (j t) -> p j t", t=PACK),
+                in0=saved[e][:, :, within * P : (within + 1) * P].rearrange("p t j -> p j t"),
                 scalar=0.0,
                 in1=turned[:].rearrange("p t j -> p j t"),
                 op0=MAX,
                 op1=MULT,
             )
 
-        def quantise(first, count):
-            e, place = divmod(first, C)
-            cols = slice(place, place + count)
-            nc.vector.quantize_mx(
-                out=dh_codes[e][:, cols].bitcast(FP8X4),
-                scales=dh_bytes[e][:, cols],
-                in_=dh[e][:, PACK * place : PACK * (place + count)],
-            )
+        def quantise(e):
+            nc.vector.quantize_mx(out=dh_codes[e][:].bitcast(FP8X4), scales=dh_bytes[e][:], in_=dh[e][:])
 
         by_token = [[keep.tile([P, T], F32, name=f"by_token{kt}{m}", align_bytes=64) for m in range(2)] for kt in range(K_TILES)]
         lists = (own_list, partner_list)
 
-        def product(grads, kt, m, first, count):
-            e, place = divmod(first, C)
-            rows = slice(kt * P, (kt + 1) * P)
-            if m == OWN:
-                codes, scales = w1_codes[:, e, rows].bitcast(FP8X4), w1_bytes[4 * e :, rows]
-            else:
-                codes, scales = wp_codes[:, e, 2 * kt * P : 2 * (kt + 1) * P].bitcast(FP4X4), wp_bytes[:, e, rows]
-            nc.tensor.matmul_mx(
-                out=grads,
-                lhsT=codes,
-                lhsT_scale=scales,
-                rhs=dh_codes[e][:, place : place + count].bitcast(FP8X4),
-                rhs_scale=dh_bytes[e][:, place : place + count],
-                start=True,
-                stop=True,
-            )
-
-        def to_sbuf(grads, name, on_vector):
-            piece = keep.tile(list(grads.shape), F32, name=name, align_bytes=64)
+        def piece(e, m, first_tile, number, on_vector):
+            grads = bank(number, [P, 2 * C])
+            for place in range(2):
+                kt = first_tile + place
+                rows = slice(kt * P, (kt + 1) * P)
+                if m == OWN:
+                    codes, scales = w1_codes[e][:, rows].bitcast(FP8X4), w1_bytes[4 * e :, rows]
+                else:
+                    codes, scales = wp_codes[:, e, 2 * kt * P : 2 * (kt + 1) * P].bitcast(FP4X4), wp_bytes[:, e, rows]
+                nc.tensor.matmul_mx(
+                    out=grads[:, place * C : (place + 1) * C],
+                    lhsT=codes,
+                    lhsT_scale=scales,
+                    rhs=dh_codes[e][:].bitcast(FP8X4),
+                    rhs_scale=dh_bytes[e][:],
+                    start=True,
+                    stop=True,
+                )
+            values = keep.tile([P, 2 * C], F32, name=f"piece{e}{m}{first_tile}", align_bytes=64)
             if on_vector:
-                nc.vector.tensor_copy(piece[:], grads[:])
+                nc.vector.tensor_copy(values[:], grads[:])
             else:
-                nc.scalar.copy(out=piece[:], in_=grads[:])
-            return piece
+                nc.scalar.copy(out=values[:], in_=grads[:])
+            return values
 
-        def scatter(values, kt, m, first, count, on_vector):
-            window = by_token[kt][m][:].indirect(lists[m][:, list_cols(first, count)])
-            if on_vector:
-                nc.vector.tensor_copy(window, values)
+        def scatter(values, e, m, kt):
+            window = by_token[kt][m][:].indirect(lists[m][:, list_cols(e * C, C)])
+            part = values[:, (kt % 2) * C : (kt % 2 + 1) * C]
+            if m == PARTNER:
+                nc.vector.tensor_copy(window, part)
             else:
-                nc.scalar.activation(out=window, in_=values, func=COPY)
-
-        def early(number, m, tiles, on_vector):
-            grads = bank(number, [P, len(tiles) * P])
-            for place, kt in enumerate(tiles):
-                product(grads[:, place * P : (place + 1) * P], kt, m, 0, P)
-            piece = to_sbuf(grads, f"early{m}{tiles[0]}", on_vector)
-            for place, kt in enumerate(tiles):
-                scatter(piece[:, place * P : (place + 1) * P], kt, m, 0, P, on_vector)
-
-        def late(number, m, kt, on_vector):
-            grads = bank(number, [P, SLOTS - P])
-            product(grads[:, 0 : C - P], kt, m, P, C - P)
-            product(grads[:, C - P :], kt, m, C, C)
-            return to_sbuf(grads, f"late{m}{kt}", on_vector)
+                nc.scalar.activation(out=window, in_=part, func=COPY)
 
         def add_on_gpsimd(kt):
             total = keep.tile([P, T], F32, name=f"total{kt}", align_bytes=64)
@@ -249,30 +216,28 @@ def tile_moe_dub_relu2_kernel(
                 nc.vector.tensor_tensor(total[:, cols], by_token[kt][OWN][:, cols], by_token[kt][PARTNER][:, cols], ADD)
                 nc.sync.dma_start(out=out[kt * P : (kt + 1) * P, cols], in_=total[:, cols])
 
-        gated0 = gated_sums(0, [0, 1])
-        turned0 = turn(gated0, 4)
-        gated1 = gated_sums(1, [2])
-        gated2 = gated_sums(2, [1])
-        gated3 = gated_sums(3, [3])
-        mask(0, turned0)
-        quantise(0, P)
-        turned1 = turn(gated1, 4)
-        early(7, OWN, (0, 1), False)
-        early(5, OWN, (2,), False)
-        mask(1, turned1)
-        quantise(P, P)
-        early(6, OWN, (3,), True)
-        mask(2, turn(gated2, 7))
-        mask(3, turn(gated3, 6))
-        quantise(C, C)
-        early(0, PARTNER, (0,), False)
-        early(6, PARTNER, (1, 2, 3), True)
-        own_banks, partner_banks = (5, 4, 7, 0), (1, 2, 3, 6)
-        partners = [late(partner_banks[kt], PARTNER, kt, kt == LAST) for kt in range(K_TILES)]
-        owns = [late(own_banks[kt], OWN, kt, False) for kt in range(K_TILES)]
-        for kt, (own, partner) in enumerate(zip(owns, partners)):
-            scatter(own[:], kt, OWN, P, SLOTS - P, False)
-            scatter(partner[:], kt, PARTNER, P, SLOTS - P, True)
+        gated = [gated_sums(c, c, (pass0[c][:], pass1[:, c * P : (c + 1) * P]), bytes0) for c in range(2)]
+        bytes1 = gather(U8, "bytes1", dy_bytes[:], C, C, "g01")
+        masked(0, gated[0], 4)
+        masked(1, gated[1], 5)
+        quantise(0)
+        gated = [gated_sums(2 + c, (1, 4)[c], (late0[:, c * P : (c + 1) * P], late1[:, c * P : (c + 1) * P]), bytes1) for c in range(2)]
+        own = [piece(0, OWN, 0, 6, False)]
+        masked(2, gated[0], 0)
+        masked(3, gated[1], 2)
+        quantise(1)
+        own.append(piece(0, OWN, 2, 7, False))
+        partner = [piece(0, PARTNER, 0, 3, True), piece(0, PARTNER, 2, 5, True)]
+        for kt in range(K_TILES):
+            scatter(own[kt // 2], 0, OWN, kt)
+            scatter(partner[kt // 2], 0, PARTNER, kt)
+        own = [piece(1, OWN, 0, 1, False)]
+        partner = [piece(1, PARTNER, 0, 4, False)]
+        own.append(piece(1, OWN, 2, 0, False))
+        partner.append(piece(1, PARTNER, 2, 2, True))
+        for kt in range(K_TILES):
+            scatter(own[kt // 2], 1, OWN, kt)
+            scatter(partner[kt // 2], 1, PARTNER, kt)
             if kt < LAST:
                 add_on_gpsimd(kt)
             else:

@@ -121,8 +121,10 @@ def tile_moe_dub_relu2_kernel(
         late1 = gather(U32, "late1", words[:, T:], C, C, "late1")
 
         dh = [keep.tile([P, C * PACK], BF16, name=f"dh{e}", align_bytes=64) for e in range(E)]
-        dh_codes = [keep.tile([P, C], U32, name=f"dh_codes{e}", align_bytes=64) for e in range(E)]
-        dh_bytes = [keep.tile([P, C], U8, name=f"dh_bytes{e}", align_bytes=64) for e in range(E)]
+        woven = keep.tile([P, C, PACK], F32, name="woven", align_bytes=64)
+        by_slot = [woven[:], saved[1][:].rearrange("p t j -> p j t")]
+        dh_codes = [keep.tile([P, C], U32, name=f"dh_codes{e}", tag=f"dh_codes{e}", align_bytes=64) for e in range(E)]
+        dh_bytes = [keep.tile([P, C], U8, name=f"dh_bytes{e}", tag=f"dh_bytes{e}", align_bytes=64) for e in range(E)]
 
         def gated_sums(c, number, codes, scales):
             e, within = divmod(c, C // P)
@@ -158,7 +160,7 @@ def tile_moe_dub_relu2_kernel(
                 nc.tensor.transpose(turned[:, t, :], gated[:, t, :], identity[:])
             nc.vector.scalar_tensor_tensor(
                 out=dh[e][:, within * P * PACK : (within + 1) * P * PACK].rearrange("p (j t) -> p j t", t=PACK),
-                in0=saved[e][:, :, within * P : (within + 1) * P].rearrange("p t j -> p j t"),
+                in0=by_slot[e][:, within * P : (within + 1) * P, :],
                 scalar=0.0,
                 in1=turned[:].rearrange("p t j -> p j t"),
                 op0=MAX,
@@ -168,12 +170,12 @@ def tile_moe_dub_relu2_kernel(
         def quantise(e):
             nc.vector.quantize_mx(out=dh_codes[e][:].bitcast(FP8X4), scales=dh_bytes[e][:], in_=dh[e][:])
 
-        by_token = [[keep.tile([P, T], F32, name=f"by_token{kt}{m}", align_bytes=64) for m in range(2)] for kt in range(K_TILES)]
+        by_token = {}
         lists = (own_list, partner_list)
 
-        def piece(e, m, first_tile, number, on_vector):
-            grads = bank(number, [P, 2 * C])
-            for place in range(2):
+        def piece(e, m, first_tile, number, on_vector, tiles=2):
+            grads = bank(number, [P, tiles * C])
+            for place in range(tiles):
                 kt = first_tile + place
                 rows = slice(kt * P, (kt + 1) * P)
                 if m == OWN:
@@ -189,16 +191,18 @@ def tile_moe_dub_relu2_kernel(
                     start=True,
                     stop=True,
                 )
-            values = keep.tile([P, 2 * C], F32, name=f"piece{e}{m}{first_tile}", align_bytes=64)
+            values = keep.tile([P, tiles * C], F32, name=f"piece{e}{m}{first_tile}", align_bytes=64)
             if on_vector:
                 nc.vector.tensor_copy(values[:], grads[:])
             else:
                 nc.scalar.copy(out=values[:], in_=grads[:])
-            return values
+            return [values[:, place * C : (place + 1) * C] for place in range(tiles)]
 
-        def scatter(values, e, m, kt):
-            window = by_token[kt][m][:].indirect(lists[m][:, list_cols(e * C, C)])
-            part = values[:, (kt % 2) * C : (kt % 2 + 1) * C]
+        def scatter(part, e, m, kt):
+            if (kt, m) not in by_token:
+                tag = {(1, OWN): "dh_codes0", (1, PARTNER): "dh_bytes0", (LAST, PARTNER): "dh_codes1"}.get((kt, m), f"window{kt}{m}")
+                by_token[kt, m] = keep.tile([P, T], F32, name=f"by_token{kt}{m}", tag=tag, align_bytes=64)
+            window = by_token[kt, m][:].indirect(lists[m][:, list_cols(e * C, C)])
             if m == PARTNER:
                 nc.vector.tensor_copy(window, part)
             else:
@@ -206,38 +210,43 @@ def tile_moe_dub_relu2_kernel(
 
         def add_on_gpsimd(kt):
             total = keep.tile([P, T], F32, name=f"total{kt}", align_bytes=64)
-            nc.gpsimd.tensor_tensor(total[:], by_token[kt][OWN][:], by_token[kt][PARTNER][:], ADD)
+            nc.gpsimd.tensor_tensor(total[:], by_token[kt, OWN][:], by_token[kt, PARTNER][:], ADD)
             nc.sync.dma_start(out=out[kt * P : (kt + 1) * P, :], in_=total[:])
 
         def add_on_vector(kt):
             total = keep.tile([P, T], F32, name=f"total{kt}", align_bytes=64)
             for side in range(2):
                 cols = slice(side * T // 2, (side + 1) * T // 2)
-                nc.vector.tensor_tensor(total[:, cols], by_token[kt][OWN][:, cols], by_token[kt][PARTNER][:, cols], ADD)
+                nc.vector.tensor_tensor(total[:, cols], by_token[kt, OWN][:, cols], by_token[kt, PARTNER][:, cols], ADD)
                 nc.sync.dma_start(out=out[kt * P : (kt + 1) * P, cols], in_=total[:, cols])
 
         gated = [gated_sums(c, c, (pass0[c][:], pass1[:, c * P : (c + 1) * P]), bytes0) for c in range(2)]
         bytes1 = gather(U8, "bytes1", dy_bytes[:], C, C, "g01")
+        nc.vector.tensor_copy(woven[:], saved[0][:].rearrange("p t j -> p j t"))
         masked(0, gated[0], 4)
         masked(1, gated[1], 5)
         quantise(0)
         gated = [gated_sums(2 + c, (1, 4)[c], (late0[:, c * P : (c + 1) * P], late1[:, c * P : (c + 1) * P]), bytes1) for c in range(2)]
-        own = [piece(0, OWN, 0, 6, False)]
+        own = piece(0, OWN, 0, 6, False)
+        partner = piece(0, PARTNER, 0, 3, True) + piece(0, PARTNER, 2, 5, True)
         masked(2, gated[0], 0)
         masked(3, gated[1], 2)
         quantise(1)
-        own.append(piece(0, OWN, 2, 7, False))
-        partner = [piece(0, PARTNER, 0, 3, True), piece(0, PARTNER, 2, 5, True)]
+        own = own + piece(0, OWN, 2, 7, False)
         for kt in range(K_TILES):
-            scatter(own[kt // 2], 0, OWN, kt)
-            scatter(partner[kt // 2], 0, PARTNER, kt)
-        own = [piece(1, OWN, 0, 1, False)]
-        partner = [piece(1, PARTNER, 0, 4, False)]
-        own.append(piece(1, OWN, 2, 0, False))
-        partner.append(piece(1, PARTNER, 2, 2, True))
+            scatter(own[kt], 0, OWN, kt)
+        for kt in range(LAST):
+            scatter(partner[kt], 0, PARTNER, kt)
+        held = partner[LAST]
+        partner = piece(1, PARTNER, 0, 6, True, 1)
+        own = piece(1, OWN, 0, 1, False)
+        partner = partner + piece(1, PARTNER, 1, 4, False, 1)
+        own = own + piece(1, OWN, 2, 0, False)
+        partner = partner + piece(1, PARTNER, 2, 2, False)
+        scatter(held, 0, PARTNER, LAST)
         for kt in range(K_TILES):
-            scatter(own[kt // 2], 1, OWN, kt)
-            scatter(partner[kt // 2], 1, PARTNER, kt)
+            scatter(own[kt], 1, OWN, kt)
+            scatter(partner[kt], 1, PARTNER, kt)
             if kt < LAST:
                 add_on_gpsimd(kt)
             else:

@@ -200,7 +200,7 @@ def tile_moe_dub_relu2_kernel(
 
         def scatter(part, e, m, kt):
             if (kt, m) not in by_token:
-                tag = {(1, OWN): "dh_codes0", (1, PARTNER): "dh_bytes0", (LAST, PARTNER): "dh_codes1"}.get((kt, m), f"window{kt}{m}")
+                tag = {(1, OWN): "dh_codes0", (1, PARTNER): "dh_bytes0", (LAST, OWN): "dh_codes1"}.get((kt, m), f"window{kt}{m}")
                 by_token[kt, m] = keep.tile([P, T], F32, name=f"by_token{kt}{m}", tag=tag, align_bytes=64)
             window = by_token[kt, m][:].indirect(lists[m][:, list_cols(e * C, C)])
             if m == PARTNER:
@@ -235,15 +235,11 @@ def tile_moe_dub_relu2_kernel(
         own = own + piece(0, OWN, 2, 7, False)
         for kt in range(K_TILES):
             scatter(own[kt], 0, OWN, kt)
-        for kt in range(LAST):
             scatter(partner[kt], 0, PARTNER, kt)
-        held = partner[LAST]
-        partner = piece(1, PARTNER, 0, 6, True, 1)
+        partner = piece(1, PARTNER, 0, 4, False)
         own = piece(1, OWN, 0, 1, False)
-        partner = partner + piece(1, PARTNER, 1, 4, False, 1)
         own = own + piece(1, OWN, 2, 0, False)
         partner = partner + piece(1, PARTNER, 2, 2, False)
-        scatter(held, 0, PARTNER, LAST)
         for kt in range(K_TILES):
             scatter(own[kt], 1, OWN, kt)
             scatter(partner[kt], 1, PARTNER, kt)

@@ -118,7 +118,6 @@ def tile_moe_dub_relu2_kernel(
         bytes0 = gather(U8, "bytes0", dy_bytes[:], 0, C, "bytes0")
         pass1 = gather(U32, "g1", words[:, T:], 0, C, "g1")
         late0 = gather(U32, "late0", words, C, C, "late0")
-        late1 = gather(U32, "late1", words[:, T:], C, C, "late1")
 
         dh = [keep.tile([P, C * PACK], BF16, name=f"dh{e}", align_bytes=64) for e in range(E)]
         woven = keep.tile([P, C, PACK], F32, name="woven", align_bytes=64)
@@ -126,31 +125,35 @@ def tile_moe_dub_relu2_kernel(
         dh_codes = [keep.tile([P, C], U32, name=f"dh_codes{e}", tag=f"dh_codes{e}", align_bytes=64) for e in range(E)]
         dh_bytes = [keep.tile([P, C], U8, name=f"dh_bytes{e}", tag=f"dh_bytes{e}", align_bytes=64) for e in range(E)]
 
-        def gated_sums(c, number, codes, scales):
+        def gated_sums(c, numbers, codes, scales):
             e, within = divmod(c, C // P)
             cols = slice(within * P, (within + 1) * P)
             gated = keep.tile([P, PACK, P], F32, name=f"gated{c}", align_bytes=64)
-            sums = bank(number, [P, H])[:]
+            width = H // len(numbers)
+            parts = [bank(number, [P, width]) for number in numbers]
             for s in range(PASSES):
-                nc.tensor.matmul_mx(
-                    out=sums,
-                    lhsT=codes[s].bitcast(FP8X4),
-                    lhsT_scale=scales[4 * s :, cols],
-                    rhs=w2_codes[e][s].bitcast(FP8X4),
-                    rhs_scale=w2_bytes[4 * (PASSES * e + s) :, :],
-                    start=(s == 0),
-                    stop=(s == PASSES - 1),
-                )
+                for part, sums in enumerate(parts):
+                    hidden = slice(part * width, (part + 1) * width)
+                    nc.tensor.matmul_mx(
+                        out=sums[:],
+                        lhsT=codes[s].bitcast(FP8X4),
+                        lhsT_scale=scales[4 * s :, cols],
+                        rhs=w2_codes[e][s][:, hidden].bitcast(FP8X4),
+                        rhs_scale=w2_bytes[4 * (PASSES * e + s) :, hidden],
+                        start=(s == 0),
+                        stop=(s == PASSES - 1),
+                    )
             if c == 0:
                 gate_cols = keep.tile([P, 32], F32, name="gate_cols", tag="g00", align_bytes=64)
                 nc.vector.transpose(gate_cols[:], gate_rows[:])
                 nc.scalar.mul(gate_twice[:], gate_cols[:, 0 : SLOTS // P], 2.0)
-            nc.scalar.activation(
-                out=gated[:],
-                in_=sums.rearrange("j (m t) -> j t m", t=PACK),
-                func=COPY,
-                scale=gate_twice[:, c : c + 1],
-            )
+            for part, sums in enumerate(parts):
+                nc.scalar.activation(
+                    out=gated[:, :, part * width // PACK : (part + 1) * width // PACK],
+                    in_=sums[:].rearrange("j (m t) -> j t m", t=PACK),
+                    func=COPY,
+                    scale=gate_twice[:, c : c + 1],
+                )
             return gated
 
         def masked(c, gated, number):
@@ -220,13 +223,14 @@ def tile_moe_dub_relu2_kernel(
                 nc.vector.tensor_tensor(total[:, cols], by_token[kt, OWN][:, cols], by_token[kt, PARTNER][:, cols], ADD)
                 nc.sync.dma_start(out=out[kt * P : (kt + 1) * P, cols], in_=total[:, cols])
 
-        gated = [gated_sums(c, c, (pass0[c][:], pass1[:, c * P : (c + 1) * P]), bytes0) for c in range(2)]
+        gated = [gated_sums(c, ((0, 2), (1,))[c], (pass0[c][:], pass1[:, c * P : (c + 1) * P]), bytes0) for c in range(2)]
+        late1 = gather(U32, "late1", words[:, T:], C, C, "gate_rows")
         bytes1 = gather(U8, "bytes1", dy_bytes[:], C, C, "g01")
         nc.vector.tensor_copy(woven[:], saved[0][:].rearrange("p t j -> p j t"))
         masked(0, gated[0], 4)
         masked(1, gated[1], 5)
         quantise(0)
-        gated = [gated_sums(2 + c, (1, 4)[c], (late0[:, c * P : (c + 1) * P], late1[:, c * P : (c + 1) * P]), bytes1) for c in range(2)]
+        gated = [gated_sums(2 + c, ((1,), (4,))[c], (late0[:, c * P : (c + 1) * P], late1[:, c * P : (c + 1) * P]), bytes1) for c in range(2)]
         own = piece(0, OWN, 0, 6, False)
         partner = piece(0, PARTNER, 0, 3, True) + piece(0, PARTNER, 2, 5, True)
         masked(2, gated[0], 0)

@@ -45,17 +45,18 @@ def tile_moe_dub_relu2_kernel(
         w2_second = keep.tile([P, PASSES, H], I32, name="w2_second", align_bytes=64)
         w2_codes = [[w2_first[s][:] for s in range(PASSES)], [w2_second[:, s, :] for s in range(PASSES)]]
         w2_bytes = keep.tile([P, H], U8, name="w2_bytes", align_bytes=64)
-        w1_codes = [keep.tile([P, K], I32, name=f"w1_codes{e}", align_bytes=64) for e in range(E)]
+        w1_codes = [keep.tile([P, K], I32, name=f"w1_codes{e}", tag=f"w1_codes{e}", align_bytes=64) for e in range(E)]
         w1_bytes = keep.tile([P, K], U8, name="w1_bytes", align_bytes=64)
         wp_codes = keep.tile([P, E, 2 * K], U8, name="wp_codes", align_bytes=64)
         wp_bytes = keep.tile([P, E, K], U8, name="wp_bytes", align_bytes=64)
         saved = [keep.tile([P, PACK, C], F32, name=f"saved{e}", align_bytes=64) for e in range(E)]
         gate_rows = keep.tile([P, 32], F32, name="gate_rows", tag="gate_rows", align_bytes=64)
-        gate_twice = keep.tile([P, SLOTS // P], F32, name="gate_twice")
+        gate_twice = keep.tile([P, 32], F32, name="gate_twice", tag="gate_twice", align_bytes=64)
         identity = keep.tile([P, P], F32, name="identity", align_bytes=64)
 
         nc.gpsimd.memset(dy_bytes[:].bitcast(I32), 0)
         nc.gpsimd.dma_start(out=gate_rows[:], in_=gate[0:8, :].rearrange("o (c q x) -> q (o c) x", c=4, q=4))
+        nc.scalar.mul(gate_twice[:], gate_rows[:], 2.0)
         make_identity(nc, identity[:])
         nc.gpsimd.memset(wp_bytes[:].rearrange("p e k -> p (e k)").bitcast(I32), 0)
         wp_rows = wpt_scales.rearrange("e s b k -> b (e s) k")
@@ -119,16 +120,18 @@ def tile_moe_dub_relu2_kernel(
         pass1 = gather(U32, "g1", words[:, T:], 0, C, "g1")
         late0 = gather(U32, "late0", words, C, C, "late0")
 
-        dh = [keep.tile([P, C * PACK], BF16, name=f"dh{e}", align_bytes=64) for e in range(E)]
+        dh = [keep.tile([P, C * PACK], BF16, name=f"dh{e}", tag=f"dh{e}", align_bytes=64) for e in range(E)]
         woven = keep.tile([P, C, PACK], F32, name="woven", align_bytes=64)
         by_slot = [woven[:], saved[1][:].rearrange("p t j -> p j t")]
         dh_codes = [keep.tile([P, C], U32, name=f"dh_codes{e}", tag=f"dh_codes{e}", align_bytes=64) for e in range(E)]
         dh_bytes = [keep.tile([P, C], U8, name=f"dh_bytes{e}", tag=f"dh_bytes{e}", align_bytes=64) for e in range(E)]
 
+        gates = []
+
         def gated_sums(c, numbers, codes, scales):
             e, within = divmod(c, C // P)
             cols = slice(within * P, (within + 1) * P)
-            gated = keep.tile([P, PACK, P], F32, name=f"gated{c}", align_bytes=64)
+            gated = keep.tile([P, PACK, P], F32, name=f"gated{c}", tag=f"gated{c}", align_bytes=64)
             width = H // len(numbers)
             parts = [bank(number, [P, width]) for number in numbers]
             for s in range(PASSES):
@@ -145,14 +148,14 @@ def tile_moe_dub_relu2_kernel(
                     )
             if c == 0:
                 gate_cols = keep.tile([P, 32], F32, name="gate_cols", tag="g00", align_bytes=64)
-                nc.vector.transpose(gate_cols[:], gate_rows[:])
-                nc.scalar.mul(gate_twice[:], gate_cols[:, 0 : SLOTS // P], 2.0)
+                nc.vector.transpose(gate_cols[:], gate_twice[:])
+                gates.append(gate_cols)
             for part, sums in enumerate(parts):
                 nc.scalar.activation(
                     out=gated[:, :, part * width // PACK : (part + 1) * width // PACK],
                     in_=sums[:].rearrange("j (m t) -> j t m", t=PACK),
                     func=COPY,
-                    scale=gate_twice[:, c : c + 1],
+                    scale=gates[0][:, c : c + 1],
                 )
             return gated
 
@@ -203,7 +206,7 @@ def tile_moe_dub_relu2_kernel(
 
         def scatter(part, e, m, kt):
             if (kt, m) not in by_token:
-                tag = {(1, OWN): "dh_codes0", (1, PARTNER): "dh_bytes0", (LAST, OWN): "dh_codes1"}.get((kt, m), f"window{kt}{m}")
+                tag = {(1, OWN): "w1_codes0", (0, PARTNER): "gated3", (1, PARTNER): "dh1", (LAST, PARTNER): "dh_codes1"}.get((kt, m), f"window{kt}{m}")
                 by_token[kt, m] = keep.tile([P, T], F32, name=f"by_token{kt}{m}", tag=tag, align_bytes=64)
             window = by_token[kt, m][:].indirect(lists[m][:, list_cols(e * C, C)])
             if m == PARTNER:
@@ -223,27 +226,32 @@ def tile_moe_dub_relu2_kernel(
                 nc.vector.tensor_tensor(total[:, cols], by_token[kt, OWN][:, cols], by_token[kt, PARTNER][:, cols], ADD)
                 nc.sync.dma_start(out=out[kt * P : (kt + 1) * P, cols], in_=total[:, cols])
 
-        gated = [gated_sums(c, ((0, 2), (1,))[c], (pass0[c][:], pass1[:, c * P : (c + 1) * P]), bytes0) for c in range(2)]
-        late1 = gather(U32, "late1", words[:, T:], C, C, "gate_rows")
+        gated = [gated_sums(c, ((0, 2), (1, 3))[c], (pass0[c][:], pass1[:, c * P : (c + 1) * P]), bytes0) for c in range(2)]
+        late1 = gather(U32, "late1", words[:, T:], C, C, "gate_twice")
         bytes1 = gather(U8, "bytes1", dy_bytes[:], C, C, "g01")
         nc.vector.tensor_copy(woven[:], saved[0][:].rearrange("p t j -> p j t"))
         masked(0, gated[0], 4)
         masked(1, gated[1], 5)
         quantise(0)
-        gated = [gated_sums(2 + c, ((1,), (4,))[c], (late0[:, c * P : (c + 1) * P], late1[:, c * P : (c + 1) * P]), bytes1) for c in range(2)]
-        own = piece(0, OWN, 0, 6, False)
-        partner = piece(0, PARTNER, 0, 3, True) + piece(0, PARTNER, 2, 5, True)
+        gated = [gated_sums(2 + c, ((1, 3), (4,))[c], (late0[:, c * P : (c + 1) * P], late1[:, c * P : (c + 1) * P]), bytes1) for c in range(2)]
         masked(2, gated[0], 0)
-        masked(3, gated[1], 2)
-        quantise(1)
+        own = piece(0, OWN, 0, 6, False)
+        partner = piece(0, PARTNER, 0, 5, True)
         own = own + piece(0, OWN, 2, 7, False)
+        masked(3, gated[1], 0)
+        quantise(1)
+        partner = partner + piece(0, PARTNER, 2, 0, True)
         for kt in range(K_TILES):
             scatter(own[kt], 0, OWN, kt)
+        for kt in range(LAST):
             scatter(partner[kt], 0, PARTNER, kt)
-        partner = piece(1, PARTNER, 0, 4, False)
+        held = partner[LAST]
+        partner = piece(1, PARTNER, 0, 6, True, 1)
         own = piece(1, OWN, 0, 1, False)
-        own = own + piece(1, OWN, 2, 0, False)
+        partner = partner + piece(1, PARTNER, 1, 4, False, 1)
+        own = own + piece(1, OWN, 2, 3, False)
         partner = partner + piece(1, PARTNER, 2, 2, False)
+        scatter(held, 0, PARTNER, LAST)
         for kt in range(K_TILES):
             scatter(own[kt], 1, OWN, kt)
             scatter(partner[kt], 1, PARTNER, kt)

@@ -26,6 +26,7 @@ PASSES = N // (P * PACK)
 K_TILES = K // P
 LAST = K_TILES - 1
 PER_COL = 16
+WARM_WIDTHS = (512, 256)
 OWN, PARTNER = 0, 1
 
 
@@ -89,8 +90,8 @@ def tile_moe_dub_relu2_kernel(
         nc.sync.dma_start(own_list[:], offs)
         load_dy(0)
         load_planes(dy_bytes, dy_scales)
-        load_dy(1)
         nc.sync.dma_start(out=w2_codes[0][0], in_=w2t_words[0, 0].rearrange("p i d -> p (i d)").bitcast(I32))
+        load_dy(1)
         load_planes(w2_bytes, w2t_scales.rearrange("e s b i -> (e s) b i"))
         nc.sync.dma_start(out=w2_codes[0][1], in_=w2t_words[0, 1].rearrange("p i d -> p (i d)").bitcast(I32))
         load_saved(0)
@@ -113,6 +114,18 @@ def tile_moe_dub_relu2_kernel(
             picked = keep.tile([P, count], dtype, name=name, tag=tag, align_bytes=64)
             nc.vector.tensor_copy(picked[:], window.indirect(own_list[:, list_cols(first, count)]))
             return picked
+
+        for width in WARM_WIDTHS:
+            unread = bank(7, [P, width])
+            nc.tensor.matmul_mx(
+                out=unread[:],
+                lhsT=w2_first[0][:, 0:P].bitcast(FP8X4),
+                lhsT_scale=w2_first[0][:].bitcast(U8)[:, 0:P],
+                rhs=w2_first[0][:, 0:width].bitcast(FP8X4),
+                rhs_scale=w2_first[0][:].bitcast(U8)[:, 0:width],
+                start=True,
+                stop=True,
+            )
 
         words = dy_codes[:].bitcast(U32)
         pass0 = [gather(U32, f"g0{c}", words[:, 0:T], c * P, P, f"g0{c}") for c in range(2)]

@@ -130,12 +130,11 @@ def tile_moe_dub_relu2_kernel(
         words = dy_codes[:].bitcast(U32)
         pass0 = [gather(U32, f"g0{c}", words[:, 0:T], c * P, P, f"g0{c}") for c in range(2)]
         bytes0 = gather(U8, "bytes0", dy_bytes[:], 0, C, "bytes0")
+        late0 = gather(U32, "late0", words[:, 0:T], C, C, "late0")
         pass1 = gather(U32, "g1", words[:, T:], 0, C, "g1")
-        late0 = gather(U32, "late0", words, C, C, "late0")
 
         dh = [keep.tile([P, C * PACK], BF16, name=f"dh{e}", tag=f"dh{e}", align_bytes=64) for e in range(E)]
-        woven = keep.tile([P, C, PACK], F32, name="woven", align_bytes=64)
-        by_slot = [woven[:], saved[1][:].rearrange("p t j -> p j t")]
+        by_slot = [saved[e][:].rearrange("p t j -> p j t") for e in range(E)]
         dh_codes = [keep.tile([P, C], U32, name=f"dh_codes{e}", tag=f"dh_codes{e}", align_bytes=64) for e in range(E)]
         dh_bytes = [keep.tile([P, C], U8, name=f"dh_bytes{e}", tag=f"dh_bytes{e}", align_bytes=64) for e in range(E)]
 
@@ -242,7 +241,6 @@ def tile_moe_dub_relu2_kernel(
         gated = [gated_sums(c, ((0, 2), (1, 3))[c], (pass0[c][:], pass1[:, c * P : (c + 1) * P]), bytes0) for c in range(2)]
         late1 = gather(U32, "late1", words[:, T:], C, C, "gate_twice")
         bytes1 = gather(U8, "bytes1", dy_bytes[:], C, C, "g01")
-        nc.vector.tensor_copy(woven[:], saved[0][:].rearrange("p t j -> p j t"))
         masked(0, gated[0], 4)
         masked(1, gated[1], 5)
         quantise(0)

@@ -132,6 +132,7 @@ def tile_moe_dub_relu2_kernel(
         bytes0 = gather(U8, "bytes0", dy_bytes[:], 0, C, "bytes0")
         late0 = gather(U32, "late0", words[:, 0:T], C, C, "late0")
         pass1 = gather(U32, "g1", words[:, T:], 0, C, "g1")
+        late1 = gather(U32, "late1", words[:, T:], C, C, "late1")
 
         dh = [keep.tile([P, C * PACK], BF16, name=f"dh{e}", tag=f"dh{e}", align_bytes=64) for e in range(E)]
         by_slot = [saved[e][:].rearrange("p t j -> p j t") for e in range(E)]
@@ -146,29 +147,29 @@ def tile_moe_dub_relu2_kernel(
             gated = keep.tile([P, PACK, P], F32, name=f"gated{c}", tag=f"gated{c}", align_bytes=64)
             width = H // len(numbers)
             parts = [bank(number, [P, width]) for number in numbers]
-            for s in range(PASSES):
-                for part, sums in enumerate(parts):
-                    hidden = slice(part * width, (part + 1) * width)
-                    nc.tensor.matmul_mx(
-                        out=sums[:],
-                        lhsT=codes[s].bitcast(FP8X4),
-                        lhsT_scale=scales[4 * s :, cols],
-                        rhs=w2_codes[e][s][:, hidden].bitcast(FP8X4),
-                        rhs_scale=w2_bytes[4 * (PASSES * e + s) :, hidden],
-                        start=(s == 0),
-                        stop=(s == PASSES - 1),
-                    )
+            steps = [(s, part) for s in range(PASSES) for part in range(len(parts))]
+            for s, part in steps if e == 0 else sorted(steps, key=lambda step: step[1]):
+                hidden = slice(part * width, (part + 1) * width)
+                nc.tensor.matmul_mx(
+                    out=parts[part][:],
+                    lhsT=codes[s].bitcast(FP8X4),
+                    lhsT_scale=scales[4 * s :, cols],
+                    rhs=w2_codes[e][s][:, hidden].bitcast(FP8X4),
+                    rhs_scale=w2_bytes[4 * (PASSES * e + s) :, hidden],
+                    start=(s == 0),
+                    stop=(s == PASSES - 1),
+                )
             if c == 0:
                 gate_cols = keep.tile([P, 32], F32, name="gate_cols", tag="g00", align_bytes=64)
                 nc.vector.transpose(gate_cols[:], gate_twice[:])
                 gates.append(gate_cols)
             for part, sums in enumerate(parts):
-                nc.scalar.activation(
-                    out=gated[:, :, part * width // PACK : (part + 1) * width // PACK],
-                    in_=sums[:].rearrange("j (m t) -> j t m", t=PACK),
-                    func=COPY,
-                    scale=gates[0][:, c : c + 1],
-                )
+                target = gated[:, :, part * width // PACK : (part + 1) * width // PACK]
+                source = sums[:].rearrange("j (m t) -> j t m", t=PACK)
+                if (c, part) == (0, 1):
+                    nc.vector.tensor_scalar(target, source, gates[0][:, c : c + 1], None, MULT)
+                else:
+                    nc.scalar.activation(out=target, in_=source, func=COPY, scale=gates[0][:, c : c + 1])
             return gated
 
         def masked(c, gated, number):
@@ -185,8 +186,12 @@ def tile_moe_dub_relu2_kernel(
                 op1=MULT,
             )
 
-        def quantise(e):
-            nc.vector.quantize_mx(out=dh_codes[e][:].bitcast(FP8X4), scales=dh_bytes[e][:], in_=dh[e][:])
+        def quantise(e, first, count):
+            nc.vector.quantize_mx(
+                out=dh_codes[e][:, first : first + count].bitcast(FP8X4),
+                scales=dh_bytes[e][:, first : first + count],
+                in_=dh[e][:, first * PACK : (first + count) * PACK],
+            )
 
         by_token = {}
         lists = (own_list, partner_list)
@@ -239,18 +244,18 @@ def tile_moe_dub_relu2_kernel(
                 nc.sync.dma_start(out=out[kt * P : (kt + 1) * P, cols], in_=total[:, cols])
 
         gated = [gated_sums(c, ((0, 2), (1, 3))[c], (pass0[c][:], pass1[:, c * P : (c + 1) * P]), bytes0) for c in range(2)]
-        late1 = gather(U32, "late1", words[:, T:], C, C, "gate_twice")
-        bytes1 = gather(U8, "bytes1", dy_bytes[:], C, C, "g01")
+        bytes1 = gather(U8, "bytes1", dy_bytes[:], C, C, "g1")
         masked(0, gated[0], 4)
         masked(1, gated[1], 5)
-        quantise(0)
+        for c in range(2):
+            quantise(0, c * P, P)
         gated = [gated_sums(2 + c, ((1, 3), (4,))[c], (late0[:, c * P : (c + 1) * P], late1[:, c * P : (c + 1) * P]), bytes1) for c in range(2)]
         masked(2, gated[0], 0)
-        own = piece(0, OWN, 0, 6, False)
+        own = piece(0, OWN, 0, 6, False, 1) + piece(0, OWN, 1, 2, False, 1)
         partner = piece(0, PARTNER, 0, 5, True)
         own = own + piece(0, OWN, 2, 7, False)
         masked(3, gated[1], 0)
-        quantise(1)
+        quantise(1, 0, C)
         partner = partner + piece(0, PARTNER, 2, 0, True)
         for kt in range(K_TILES):
             scatter(own[kt], 0, OWN, kt)

@@ -50,7 +50,8 @@ def tile_moe_dub_relu2_kernel(
         w1_bytes = keep.tile([P, K], U8, name="w1_bytes", align_bytes=64)
         wp_codes = keep.tile([P, E, 2 * K], U8, name="wp_codes", align_bytes=64)
         wp_bytes = keep.tile([P, E, K], U8, name="wp_bytes", align_bytes=64)
-        saved = [keep.tile([P, PACK, C], F32, name=f"saved{e}", align_bytes=64) for e in range(E)]
+        saved_first = keep.tile([P, PACK, C], F32, name="saved_first", align_bytes=64)
+        saved_late = [keep.tile([P, PACK, P], F32, name=f"saved_late{c}", align_bytes=64) for c in range(2)]
         gate_rows = keep.tile([P, 32], F32, name="gate_rows", tag="gate_rows", align_bytes=64)
         gate_twice = keep.tile([P, 32], F32, name="gate_twice", tag="gate_twice", align_bytes=64)
         identity = keep.tile([P, P], F32, name="identity", align_bytes=64)
@@ -84,8 +85,8 @@ def tile_moe_dub_relu2_kernel(
         def load_dy(s):
             nc.sync.dma_start(out=dy_codes[:, s * T : (s + 1) * T], in_=dy_words[s].rearrange("p t d -> p (t d)").bitcast(I32))
 
-        def load_saved(e):
-            nc.sync.dma_start(out=saved[e][:], in_=a[:, e * C : (e + 1) * C].rearrange("(p t) j -> p t j", t=PACK))
+        def load_saved(tile, first, count):
+            nc.sync.dma_start(out=tile[:], in_=a[:, first : first + count].rearrange("(p t) j -> p t j", t=PACK))
 
         nc.sync.dma_start(own_list[:], offs)
         load_dy(0)
@@ -94,12 +95,13 @@ def tile_moe_dub_relu2_kernel(
         load_dy(1)
         load_planes(w2_bytes, w2t_scales.rearrange("e s b i -> (e s) b i"))
         nc.sync.dma_start(out=w2_codes[0][1], in_=w2t_words[0, 1].rearrange("p i d -> p (i d)").bitcast(I32))
-        load_saved(0)
+        load_saved(saved_first, 0, C)
         nc.sync.dma_start(out=w2_second[:], in_=w2t_words[1].rearrange("s p i d -> p s (i d)").bitcast(I32))
         load_w1(0)
         load_planes(w1_bytes, w1t_scales.rearrange("e s b k -> (e s) b k"))
-        load_saved(1)
+        load_saved(saved_late[0], C, P)
         nc.sync.dma_start(out=wp_codes[:].bitcast(I32), in_=wpt_words.rearrange("e s p b -> p (e s) b").bitcast(I32))
+        load_saved(saved_late[1], C + P, P)
         nc.sync.dma_start(partner_list[:], offs2)
         load_w1(1)
 
@@ -135,7 +137,7 @@ def tile_moe_dub_relu2_kernel(
         late1 = gather(U32, "late1", words[:, T:], C, C, "late1")
 
         dh = [keep.tile([P, C * PACK], BF16, name=f"dh{e}", tag=f"dh{e}", align_bytes=64) for e in range(E)]
-        by_slot = [saved[e][:].rearrange("p t j -> p j t") for e in range(E)]
+        saved = [saved_first[:, :, 0:P], saved_first[:, :, P:], saved_late[0][:], saved_late[1][:]]
         dh_codes = [keep.tile([P, C], U32, name=f"dh_codes{e}", tag=f"dh_codes{e}", align_bytes=64) for e in range(E)]
         dh_bytes = [keep.tile([P, C], U8, name=f"dh_bytes{e}", tag=f"dh_bytes{e}", align_bytes=64) for e in range(E)]
 
@@ -179,7 +181,7 @@ def tile_moe_dub_relu2_kernel(
                 nc.tensor.transpose(turned[:, t, :], gated[:, t, :], identity[:])
             nc.vector.scalar_tensor_tensor(
                 out=dh[e][:, within * P * PACK : (within + 1) * P * PACK].rearrange("p (j t) -> p j t", t=PACK),
-                in0=by_slot[e][:, within * P : (within + 1) * P, :],
+                in0=saved[c].rearrange("p t j -> p j t"),
                 scalar=0.0,
                 in1=turned[:].rearrange("p t j -> p j t"),
                 op0=MAX,

@@ -26,7 +26,6 @@ PASSES = N // (P * PACK)
 K_TILES = K // P
 LAST = K_TILES - 1
 PER_COL = 16
-WARM_WIDTHS = (512, 256)
 OWN, PARTNER = 0, 1
 
 
@@ -116,18 +115,6 @@ def tile_moe_dub_relu2_kernel(
             picked = keep.tile([P, count], dtype, name=name, tag=tag, align_bytes=64)
             nc.vector.tensor_copy(picked[:], window.indirect(own_list[:, list_cols(first, count)]))
             return picked
-
-        for width in WARM_WIDTHS:
-            unread = bank(7, [P, width])
-            nc.tensor.matmul_mx(
-                out=unread[:],
-                lhsT=w2_first[0][:, 0:P].bitcast(FP8X4),
-                lhsT_scale=w2_first[0][:].bitcast(U8)[:, 0:P],
-                rhs=w2_first[0][:, 0:width].bitcast(FP8X4),
-                rhs_scale=w2_first[0][:].bitcast(U8)[:, 0:width],
-                start=True,
-                stop=True,
-            )
 
         words = dy_codes[:].bitcast(U32)
         pass0 = [gather(U32, f"g0{c}", words[:, 0:T], c * P, P, f"g0{c}") for c in range(2)]

from contextlib import ExitStack

import concourse.mybir as mybir
from concourse.masks import make_identity

K, T, E, C, H, N = 512, 512, 2, 256, 512, 1024
SLOTS = E * C
FLOPS = 2 * SLOTS * H * (N + 2 * K)

F32 = mybir.dt.float32
BF16 = mybir.dt.bfloat16
I32 = mybir.dt.int32
U32 = mybir.dt.uint32
U16 = mybir.dt.uint16
U8 = mybir.dt.uint8
FP8X4 = mybir.dt.float8_e4m3fn_x4
FP4X4 = mybir.dt.float4_e2m1fn_x4
COPY = mybir.ActivationFunctionType.Copy
MAX = mybir.AluOpType.max
MULT = mybir.AluOpType.mult
ADD = mybir.AluOpType.add

P = 128
PACK = 4
PASSES = N // (P * PACK)
K_TILES = K // P
LAST = K_TILES - 1
PER_COL = 16
OWN, PARTNER = 0, 1


def tile_moe_dub_relu2_kernel(
    tc, dy_words, dy_scales, w2t_words, w2t_scales, w1t_words, w1t_scales, wpt_words, wpt_scales, a, gate, offs, offs2, out
):
    nc = tc.nc
    with ExitStack() as ctx:
        keep = ctx.enter_context(tc.tile_pool(name="keep", bufs=1))
        psum = ctx.enter_context(tc.psum_pool(name="psum", bufs=1))

        own_list = keep.tile([P, SLOTS // PER_COL], U16, name="own_list")
        partner_list = keep.tile([P, SLOTS // PER_COL], U16, name="partner_list")
        dy_codes = keep.tile([P, PASSES * T], I32, name="dy_codes", align_bytes=64)
        dy_bytes = keep.tile([P, T], U8, name="dy_bytes", align_bytes=64)
        w2_first = [keep.tile([P, H], I32, name=f"w2_first{s}", align_bytes=64) for s in range(PASSES)]
        w2_second = keep.tile([P, PASSES, H], I32, name="w2_second", align_bytes=64)
        w2_codes = [[w2_first[s][:] for s in range(PASSES)], [w2_second[:, s, :] for s in range(PASSES)]]
        w2_bytes = keep.tile([P, H], U8, name="w2_bytes", align_bytes=64)
        w1_codes = [keep.tile([P, K], I32, name=f"w1_codes{e}", tag=f"w1_codes{e}", align_bytes=64) for e in range(E)]
        w1_bytes = keep.tile([P, K], U8, name="w1_bytes", align_bytes=64)
        wp_codes = keep.tile([P, E, 2 * K], U8, name="wp_codes", align_bytes=64)
        wp_bytes = keep.tile([P, E, K], U8, name="wp_bytes", align_bytes=64)
        saved_first = keep.tile([P, PACK, C], F32, name="saved_first", align_bytes=64)
        saved_late = [keep.tile([P, PACK, P], F32, name=f"saved_late{c}", align_bytes=64) for c in range(2)]
        gate_rows = keep.tile([P, 32], F32, name="gate_rows", tag="gate_rows", align_bytes=64)
        gate_twice = keep.tile([P, 32], F32, name="gate_twice", tag="gate_twice", align_bytes=64)
        identity = keep.tile([P, P], F32, name="identity", align_bytes=64)

        nc.gpsimd.memset(dy_bytes[:].bitcast(I32), 0)
        nc.gpsimd.dma_start(out=gate_rows[:], in_=gate[0:8, :].rearrange("o (c q x) -> q (o c) x", c=4, q=4))
        nc.scalar.mul(gate_twice[:], gate_rows[:], 2.0)
        make_identity(nc, identity[:])
        nc.gpsimd.memset(wp_bytes[:].rearrange("p e k -> p (e k)").bitcast(I32), 0)
        wp_rows = wpt_scales.rearrange("e s b k -> b (e s) k")
        for q in range(4):
            nc.gpsimd.dma_start(
                out=wp_bytes[32 * q : 32 * q + 4, :, :].bitcast(I32),
                in_=wp_rows[4 * q : 4 * q + 4, :, :].bitcast(I32),
            )
        nc.vector.memset(w2_bytes[:].bitcast(I32), 0)
        nc.vector.memset(w1_bytes[:].bitcast(I32), 0)

        def load_planes(plane, rows):
            count = rows.shape[0]
            for q in range(4):
                nc.sync.dma_start(
                    out=plane[32 * q : 32 * q + 4 * count, :].bitcast(I32),
                    in_=rows[:, 4 * q : 4 * q + 4, :].bitcast(I32),
                )


        def load_w1(e):
            nc.sync.dma_start(out=w1_codes[e][:], in_=w1t_words[e, 0].rearrange("p k d -> p (k d)").bitcast(I32))

        def load_dy(s):
            nc.sync.dma_start(out=dy_codes[:, s * T : (s + 1) * T], in_=dy_words[s].rearrange("p t d -> p (t d)").bitcast(I32))

        def load_saved(tile, first, count):
            nc.sync.dma_start(out=tile[:], in_=a[:, first : first + count].rearrange("(p t) j -> p t j", t=PACK))

        nc.sync.dma_start(own_list[:], offs)
        load_dy(0)
        load_planes(dy_bytes, dy_scales)
        nc.sync.dma_start(out=w2_codes[0][0], in_=w2t_words[0, 0].rearrange("p i d -> p (i d)").bitcast(I32))
        load_dy(1)
        load_planes(w2_bytes, w2t_scales.rearrange("e s b i -> (e s) b i"))
        nc.sync.dma_start(out=w2_codes[0][1], in_=w2t_words[0, 1].rearrange("p i d -> p (i d)").bitcast(I32))
        load_saved(saved_first, 0, C)
        nc.sync.dma_start(out=w2_second[:], in_=w2t_words[1].rearrange("s p i d -> p s (i d)").bitcast(I32))
        load_w1(0)
        load_planes(w1_bytes, w1t_scales.rearrange("e s b k -> (e s) b k"))
        load_saved(saved_late[0], C, P)
        nc.sync.dma_start(out=wp_codes[:].bitcast(I32), in_=wpt_words.rearrange("e s p b -> p (e s) b").bitcast(I32))
        load_saved(saved_late[1], C + P, P)
        nc.sync.dma_start(partner_list[:], offs2)
        load_w1(1)

        def bank(number, shape):
            return psum.tile(shape, F32, name=f"bank{number}")


        def list_cols(first, count):
            return slice(first // PER_COL, (first + count) // PER_COL)

        def gather(dtype, name, window, first, count, tag):
            picked = keep.tile([P, count], dtype, name=name, tag=tag, align_bytes=64)
            nc.vector.tensor_copy(picked[:], window.indirect(own_list[:, list_cols(first, count)]))
            return picked

        words = dy_codes[:].bitcast(U32)
        pass0 = [gather(U32, f"g0{c}", words[:, 0:T], c * P, P, f"g0{c}") for c in range(2)]
        bytes0 = gather(U8, "bytes0", dy_bytes[:], 0, C, "bytes0")
        late0 = gather(U32, "late0", words[:, 0:T], C, C, "late0")
        pass1 = gather(U32, "g1", words[:, T:], 0, C, "g1")
        late1 = gather(U32, "late1", words[:, T:], C, C, "late1")

        dh = [keep.tile([P, C * PACK], BF16, name=f"dh{e}", tag=f"dh{e}", align_bytes=64) for e in range(E)]
        saved = [saved_first[:, :, 0:P], saved_first[:, :, P:], saved_late[0][:], saved_late[1][:]]
        dh_codes = [keep.tile([P, C], U32, name=f"dh_codes{e}", tag=f"dh_codes{e}", align_bytes=64) for e in range(E)]
        dh_bytes = [keep.tile([P, C], U8, name=f"dh_bytes{e}", tag=f"dh_bytes{e}", align_bytes=64) for e in range(E)]

        gates = []

        def gated_sums(c, numbers, codes, scales):
            e, within = divmod(c, C // P)
            cols = slice(within * P, (within + 1) * P)
            gated = keep.tile([P, PACK, P], F32, name=f"gated{c}", tag=f"gated{c}", align_bytes=64)
            width = H // len(numbers)
            parts = [bank(number, [P, width]) for number in numbers]
            steps = [(s, part) for s in range(PASSES) for part in range(len(parts))]
            for s, part in steps if e == 0 else sorted(steps, key=lambda step: step[1]):
                hidden = slice(part * width, (part + 1) * width)
                nc.tensor.matmul_mx(
                    out=parts[part][:],
                    lhsT=codes[s].bitcast(FP8X4),
                    lhsT_scale=scales[4 * s :, cols],
                    rhs=w2_codes[e][s][:, hidden].bitcast(FP8X4),
                    rhs_scale=w2_bytes[4 * (PASSES * e + s) :, hidden],
                    start=(s == 0),
                    stop=(s == PASSES - 1),
                )
            if c == 0:
                gate_cols = keep.tile([P, 32], F32, name="gate_cols", tag="g00", align_bytes=64)
                nc.vector.transpose(gate_cols[:], gate_twice[:])
                gates.append(gate_cols)
            for part, sums in enumerate(parts):
                target = gated[:, :, part * width // PACK : (part + 1) * width // PACK]
                source = sums[:].rearrange("j (m t) -> j t m", t=PACK)
                if (c, part) == (0, 1):
                    nc.vector.tensor_scalar(target, source, gates[0][:, c : c + 1], None, MULT)
                else:
                    nc.scalar.activation(out=target, in_=source, func=COPY, scale=gates[0][:, c : c + 1])
            return gated

        def masked(c, gated, number):
            e, within = divmod(c, C // P)
            turned = bank(number, [P, PACK, P])
            for t in range(PACK):
                nc.tensor.transpose(turned[:, t, :], gated[:, t, :], identity[:])
            nc.vector.scalar_tensor_tensor(
                out=dh[e][:, within * P * PACK : (within + 1) * P * PACK].rearrange("p (j t) -> p j t", t=PACK),
                in0=saved[c].rearrange("p t j -> p j t"),
                scalar=0.0,
                in1=turned[:].rearrange("p t j -> p j t"),
                op0=MAX,
                op1=MULT,
            )

        def quantise(e, first, count):
            nc.vector.quantize_mx(
                out=dh_codes[e][:, first : first + count].bitcast(FP8X4),
                scales=dh_bytes[e][:, first : first + count],
                in_=dh[e][:, first * PACK : (first + count) * PACK],
            )

        by_token = {}
        lists = (own_list, partner_list)

        def piece(e, m, first_tile, number, on_vector, tiles=2):
            grads = bank(number, [P, tiles * C])
            for place in range(tiles):
                kt = first_tile + place
                rows = slice(kt * P, (kt + 1) * P)
                if m == OWN:
                    codes, scales = w1_codes[e][:, rows].bitcast(FP8X4), w1_bytes[4 * e :, rows]
                else:
                    codes, scales = wp_codes[:, e, 2 * kt * P : 2 * (kt + 1) * P].bitcast(FP4X4), wp_bytes[:, e, rows]
                nc.tensor.matmul_mx(
                    out=grads[:, place * C : (place + 1) * C],
                    lhsT=codes,
                    lhsT_scale=scales,
                    rhs=dh_codes[e][:].bitcast(FP8X4),
                    rhs_scale=dh_bytes[e][:],
                    start=True,
                    stop=True,
                )
            values = keep.tile([P, tiles * C], F32, name=f"piece{e}{m}{first_tile}", align_bytes=64)
            if on_vector:
                nc.vector.tensor_copy(values[:], grads[:])
            else:
                nc.scalar.copy(out=values[:], in_=grads[:])
            return [values[:, place * C : (place + 1) * C] for place in range(tiles)]

        def scatter(part, e, m, kt):
            if (kt, m) not in by_token:
                tag = {(1, OWN): "w1_codes0", (0, PARTNER): "gated3", (1, PARTNER): "dh1", (LAST, PARTNER): "dh_codes1"}.get((kt, m), f"window{kt}{m}")
                by_token[kt, m] = keep.tile([P, T], F32, name=f"by_token{kt}{m}", tag=tag, align_bytes=64)
            window = by_token[kt, m][:].indirect(lists[m][:, list_cols(e * C, C)])
            if m == PARTNER:
                nc.vector.tensor_copy(window, part)
            else:
                nc.scalar.activation(out=window, in_=part, func=COPY)

        def add_on_gpsimd(kt):
            total = keep.tile([P, T], F32, name=f"total{kt}", align_bytes=64)
            nc.gpsimd.tensor_tensor(total[:], by_token[kt, OWN][:], by_token[kt, PARTNER][:], ADD)
            nc.sync.dma_start(out=out[kt * P : (kt + 1) * P, :], in_=total[:])

        def add_on_vector(kt):
            total = keep.tile([P, T], F32, name=f"total{kt}", align_bytes=64)
            for side in range(2):
                cols = slice(side * T // 2, (side + 1) * T // 2)
                nc.vector.tensor_tensor(total[:, cols], by_token[kt, OWN][:, cols], by_token[kt, PARTNER][:, cols], ADD)
                nc.sync.dma_start(out=out[kt * P : (kt + 1) * P, cols], in_=total[:, cols])

        gated = [gated_sums(c, ((0, 2), (1, 3))[c], (pass0[c][:], pass1[:, c * P : (c + 1) * P]), bytes0) for c in range(2)]
        bytes1 = gather(U8, "bytes1", dy_bytes[:], C, C, "g1")
        masked(0, gated[0], 4)
        masked(1, gated[1], 5)
        for c in range(2):
            quantise(0, c * P, P)
        gated = [gated_sums(2 + c, ((1, 3), (4,))[c], (late0[:, c * P : (c + 1) * P], late1[:, c * P : (c + 1) * P]), bytes1) for c in range(2)]
        masked(2, gated[0], 0)
        own = piece(0, OWN, 0, 6, False, 1) + piece(0, OWN, 1, 2, False, 1)
        partner = piece(0, PARTNER, 0, 5, True)
        own = own + piece(0, OWN, 2, 7, False)
        masked(3, gated[1], 0)
        quantise(1, 0, C)
        partner = partner + piece(0, PARTNER, 2, 0, True)
        for kt in range(K_TILES):
            scatter(own[kt], 0, OWN, kt)
        for kt in range(LAST):
            scatter(partner[kt], 0, PARTNER, kt)
        held = partner[LAST]
        partner = piece(1, PARTNER, 0, 6, True, 1)
        own = piece(1, OWN, 0, 1, False)
        partner = partner + piece(1, PARTNER, 1, 4, False, 1)
        own = own + piece(1, OWN, 2, 3, False)
        partner = partner + piece(1, PARTNER, 2, 2, False)
        scatter(held, 0, PARTNER, LAST)
        for kt in range(K_TILES):
            scatter(own[kt], 1, OWN, kt)
            scatter(partner[kt], 1, PARTNER, kt)
            if kt < LAST:
                add_on_gpsimd(kt)
            else:
                add_on_vector(kt)
